import numpy as np
import ml_dtypes


def mxq(x, axis, fmt="e4m3"):
    dtype, down = {"e4m3": (ml_dtypes.float8_e4m3fn, 7), "e5m2": (ml_dtypes.float8_e5m2, 14)}[fmt]
    v = np.moveaxis(np.asarray(x, np.float32).astype(ml_dtypes.bfloat16).astype(np.float64), axis, -1)
    blocks = v.reshape(v.shape[:-1] + (-1, 32))
    amax = np.abs(blocks).max(-1, keepdims=True)
    byte = np.maximum(np.where(amax > 0, np.frexp(amax)[1] - 1 + 127, 0) - down, 1)
    scale = np.exp2(byte - 127.0)
    codes = (blocks / scale).astype(np.float32).astype(dtype).astype(np.float64)
    return np.moveaxis((codes * scale).reshape(v.shape), -1, axis)


WIDE = False


def mx_kscale(k):
    if not WIDE:
        return np.ones(k)
    levels = np.array([24, -24, 12, -12, 0])
    if k % 512:
        return np.exp2(np.random.permutation(np.resize(levels, k // 32))).repeat(32)
    a = np.empty((k // 512, 16))
    for p in range(k // 512):
        a[p, :8] = np.random.permutation(np.resize(levels, 8))
        for g in range(8):
            far = levels[np.abs(levels - a[p, g]) >= 10]
            a[p, g + 8] = far[np.random.randint(len(far))]
    return np.exp2(a.ravel()).repeat(32)


def f64(x):
    return np.asarray(x).astype(np.float64)


def striped(idx):
    return np.tile(idx.reshape(-1, 16).T, (8, 1)).astype(np.uint16)


def unstriped(offs):
    return offs[:16].T.reshape(-1).astype(np.int64)


E2M1 = np.array([0.0, 0.5, 1.0, 1.5, 2.0, 3.0, 4.0, 6.0, -0.0, -0.5, -1.0, -1.5, -2.0, -3.0, -4.0, -6.0])


def pack_weight(w, fmt):
    k, n = w.shape
    w = f64(np.asarray(w, np.float32).astype(ml_dtypes.bfloat16)).reshape(k // 32, 32, n)
    amax = np.abs(w).max(1)
    if fmt == "e4m3":
        byte = np.frexp(amax)[1] - 1 + 127 - 7
    else:
        mant, ex = np.frexp(amax / 6.0)
        byte = np.where(mant > 0.5, ex, ex - 1) + 127
    byte = np.clip(np.where(amax > 0, byte, 1), 1, 254)
    scaled = (w * np.exp2(127.0 - byte)[:, None, :]).reshape(k, n).astype(np.float32)
    by_word = np.ascontiguousarray(scaled.reshape(k // 512, 128, 4, n).transpose(0, 1, 3, 2))
    if fmt == "e4m3":
        words = by_word.astype(ml_dtypes.float8_e4m3fn).view(np.uint8)
    else:
        c = by_word.astype(ml_dtypes.float4_e2m1fn).view(np.uint8) & 0xF
        words = (c[..., 0::2] | (c[..., 1::2] << 4)).reshape(k // 512, 128, 2 * n)
    return np.ascontiguousarray(words), np.ascontiguousarray(byte.astype(np.uint8).reshape(k // 512, 16, n))


def unpack_weight(words, scales, fmt):
    g, _, n = scales.shape
    words = np.ascontiguousarray(words).reshape(g, 128, n, -1)
    if fmt == "e4m3":
        vals = words.view(ml_dtypes.float8_e4m3fn).astype(np.float64)
    else:
        nib = np.empty((g, 128, n, 4), np.uint8)
        nib[..., 0::2] = words & 0xF
        nib[..., 1::2] = words >> 4
        vals = E2M1[nib]
    vals = vals * np.repeat(np.exp2(scales.astype(np.float64) - 127.0), 8, axis=1)[..., None]
    return vals.transpose(0, 1, 3, 2).reshape(g * 512, n)


def pack_table4(v):
    words, scales = pack_weight(v, "e2m1")
    g, t = words.shape[0] // 2, v.shape[1]
    return np.ascontiguousarray(words.reshape(g, 2, 128, t, 2).transpose(0, 2, 3, 1, 4).reshape(g, 128, t, 4)), scales


def unpack_table4(words, scales):
    g, _, t, _ = words.shape
    return unpack_weight(words.reshape(g, 128, t, 2, 2).transpose(0, 3, 1, 2, 4).reshape(2 * g, 128, 2 * t), scales, "e2m1")


def planes(y):
    n, m = y.shape
    v = y.astype(np.float32).astype(ml_dtypes.bfloat16).astype(np.float64).reshape(n // 32, 32, m)
    top = np.abs(v).max(1)
    byte = np.clip(np.where(top > 0, np.frexp(top)[1] - 1 + 127 - 7, 1), 1, 254)
    codes = (v * np.exp2(127.0 - byte)[:, None, :]).reshape(n, m).astype(np.float32).astype(ml_dtypes.float8_e4m3fn).view(np.uint8)
    words = codes.reshape(n // 512, 128, 4, m).transpose(0, 1, 3, 2)
    return np.ascontiguousarray(words), np.ascontiguousarray(byte.astype(np.uint8).reshape(n // 512, 16, m))


K, R, N, T, J = 1024, 512, 512, 4096, 1024


def setup_inputs():
    n = np.random.standard_normal
    s = mx_kscale(K)[:, None]
    u = mx_kscale(R)[:, None]
    wb = 0.7 * n((K, N)) / np.sqrt(K) / s
    wb4 = pack_weight(wb, "e2m1")
    wbrest = wb - unpack_weight(*wb4, "e2m1")
    p_tab = pack_table4(n((K, T)) * s)
    p_wb8 = pack_weight(wbrest, "e4m3")
    p_dn = pack_weight(n((K, R)) / np.sqrt(K) / s * u.T, "e4m3")
    return {
        "tab_words": p_tab[0],
        "tab_scales": p_tab[1],
        "wb4_words": wb4[0],
        "wb4_scales": wb4[1],
        "wb8_words": p_wb8[0],
        "wb8_scales": p_wb8[1],
        "dn_words": p_dn[0],
        "dn_scales": p_dn[1],
        "upw": (2.0 * n((R, N)) / np.sqrt(R) / u).astype(np.float32),
        "x0T": (n((N, T))).astype(np.float32),
        "b": (0.3 * n(N)).astype(np.float32),
        "offs": striped(np.random.permutation(T)[:J]),
    }


def reference(tab_words, tab_scales, wb4_words, wb4_scales, wb8_words, wb8_scales, dn_words, dn_scales, upw, x0T, b, offs):
    idx = unstriped(offs)
    tab_ = unpack_table4(tab_words, tab_scales)[:, idx]
    wb4_ = unpack_weight(wb4_words, wb4_scales, "e2m1")
    wb8_ = unpack_weight(wb8_words, wb8_scales, "e4m3")
    dn_ = unpack_weight(dn_words, dn_scales, "e4m3")
    hs = dn_.T @ tab_
    h = np.maximum(hs, 0.0)
    h_ = mxq(h, 0, "e4m3")
    upw_ = mxq(f64(upw), 0, "e4m3")
    y = wb4_.T @ tab_ + wb8_.T @ tab_ + upw_.T @ h_
    out_0 = f64(x0T)[:, idx] * (y + f64(b)[:, None]) + f64(x0T)[:, idx]
    return (out_0,) + planes(out_0)

@@ -1,0 +1,251 @@
+from contextlib import ExitStack
+
+import concourse.mybir as mybir
+
+K, R, N, T, J = 1024, 512, 512, 4096, 1024
+FLOPS = 2 * J * (K * R + 2 * K * N + R * N)
+
+F32 = mybir.dt.float32
+BF16 = mybir.dt.bfloat16
+I32 = mybir.dt.int32
+U32 = mybir.dt.uint32
+U16 = mybir.dt.uint16
+U8 = mybir.dt.uint8
+FP8X4 = mybir.dt.float8_e4m3fn_x4
+FP4X4 = mybir.dt.float4_e2m1fn_x4
+ACT = mybir.ActivationFunctionType
+ALU = mybir.AluOpType
+
+P = 128
+PACK = 4
+PASSES = K // (P * PACK)
+HALF = 512
+HALVES = J // HALF
+HCHUNK = 128
+TAIL = 256
+LIST_ROWS = 16
+
+
+def tile_list_xcross_res_reluP_kernel(
+    tc, tab_words, tab_scales, wb4_words, wb4_scales, wb8_words, wb8_scales, dn_words, dn_scales, upw, x0T, b, offs,
+    out_0, out_1, out_2,
+):
+    nc = tc.nc
+    with ExitStack() as ctx:
+        keep = ctx.enter_context(tc.tile_pool(name="keep", bufs=1))
+        reuse = ctx.enter_context(tc.tile_pool(name="reuse", bufs=1))
+        hs_psum = ctx.enter_context(tc.psum_pool(name="hs_psum", bufs=3))
+        y_psum = ctx.enter_context(tc.psum_pool(name="y_psum", bufs=5))
+
+        def held(name, shape, dtype):
+            return keep.tile(shape, dtype, name=name, align_bytes=64)
+
+        def listed(j0, n):
+            return offsets[:, j0 // LIST_ROWS : (j0 + n) // LIST_ROWS]
+
+        def load_scale_rows(queue, plane, scales):
+            for q in range(4):
+                queue.dma_start(
+                    out=plane[32 * q : 32 * q + 4].bitcast(I32),
+                    in_=scales[:, 4 * q : 4 * q + 4, :].rearrange("a r c -> r a c").bitcast(I32),
+                )
+
+        def deal(out, in_, run):
+            nc.vector.tensor_copy(
+                out=out.rearrange("p a (t c i) -> p a c t i", t=PACK, i=run),
+                in_=in_.rearrange("p a (c i t) -> p a c t i", t=PACK, i=run),
+            )
+
+        offsets = keep.tile([P, J // LIST_ROWS], U16, name="offsets")
+        nc.sync.dma_start(offsets[:], offs)
+
+        def placed(name, shape, dtype, kib):
+            return reuse.tile(shape, dtype, name=name, align_bytes=64, offset=kib * 1024)
+
+        def scale_staging(name):
+            tile = held(name, [P, PASSES, N], U8)
+            nc.gpsimd.memset(tile[:].rearrange("p a c -> p (a c)").bitcast(I32), 0)
+            return tile
+
+        tab_s = placed("tab_s", [P, PASSES, T], U8, 1)
+        nc.vector.memset(tab_s[:].rearrange("p a t -> p (a t)").bitcast(I32), 0)
+        raw_s = []
+        for name, scales in (("dn_raw_s", dn_scales), ("wb4_raw_s", wb4_scales), ("wb8_raw_s", wb8_scales)):
+            raw_s.append(scale_staging(name))
+            load_scale_rows(nc.gpsimd, raw_s[-1], scales)
+        b_raw = held("b_raw", [P, PACK], F32)
+        nc.scalar.dma_start(out=b_raw[:], in_=b.rearrange("(p t) -> p t", t=PACK))
+
+        dn_raw = placed("dn_raw", [P, PASSES, R], I32, 37)
+        nc.sync.dma_start(out=dn_raw[:], in_=dn_words.rearrange("a p r f -> p a (r f)").bitcast(I32))
+        tab_w = placed("tab_w", [P, T], I32, 54)
+        nc.sync.dma_start(out=tab_w[:], in_=tab_words[0].rearrange("p t f -> p (t f)").bitcast(I32))
+        wb8_raw = held("wb8_raw", [P, PASSES, N], I32)
+        nc.sync.dma_start(out=wb8_raw[:], in_=wb8_words.rearrange("a p n f -> p a (n f)").bitcast(I32))
+        load_scale_rows(nc.scalar, tab_s, tab_scales)
+
+
+        v_s, v_w = [], []
+
+        def gather_scales(h):
+            s = held("v_s%d" % h, [P, PASSES, HALF], U8)
+            for a in range(PASSES):
+                nc.vector.tensor_copy(out=s[:, a, :], in_=tab_s[:, a, :].indirect(listed(h * HALF, HALF)))
+            v_s.append(s)
+
+        def gather_words(h):
+            both = placed("both", [P, HALF], U32, 0)
+            nc.vector.tensor_copy(out=both[:], in_=tab_w[:].bitcast(U32).indirect(listed(h * HALF, HALF)))
+            w = held("v_w%d" % h, [P, PASSES, 2 * HALF], U8)
+            nc.vector.tensor_copy(out=w[:].bitcast(U16), in_=both[:].bitcast(U16).rearrange("p (j a) -> p a j", a=PASSES))
+            v_w.append(w)
+
+        dn_w = held("dn_w", [P, PASSES, R], I32)
+        deal(dn_w[:], dn_raw[:], 4)
+        dn_s = held("dn_s", [P, PASSES, R], U8)
+        deal(dn_s[:], raw_s[0][:], 16)
+        wb4_raw = placed("wb4_raw", [P, PASSES, 2 * N], U8, 36)
+        nc.sync.dma_start(out=wb4_raw[:].bitcast(I32), in_=wb4_words.rearrange("a p c -> p a c").bitcast(I32))
+        up_raw = placed("up_raw", [P, PACK, N], F32, 38)
+        nc.sync.dma_start(out=up_raw[:], in_=upw.rearrange("(p i) n -> p i n", i=PACK))
+        x0 = []
+
+        def load_x0(kib):
+            t = len(x0)
+            x0.append(placed("x0_%d" % t, [P, T], F32, kib))
+            nc.sync.dma_start(out=x0[t][:], in_=x0T.rearrange("(p t) c -> p t c", t=PACK)[:, t, :])
+
+        for h in range(HALVES):
+            gather_scales(h)
+        load_x0(6)
+        gather_words(0)
+
+        h_bf = [held("h_bf%d" % h, [P, HALF, PACK], BF16) for h in range(HALVES)]
+        h_w = [held("h_w%d" % h, [P, HALF], U32) for h in range(HALVES)]
+        h_s = [held("h_s%d" % h, [P, HALF], U8) for h in range(HALVES)]
+
+        def hidden_half(h):
+            for c in range(HALF // HCHUNK):
+                hs = hs_psum.tile([P, PACK, HCHUNK], F32, name="hs")
+                for t in range(PACK):
+                    for a in range(PASSES):
+                        nc.tensor.matmul_mx(
+                            out=hs[:, t, :],
+                            lhsT=dn_w[:, a, t * P : (t + 1) * P].bitcast(FP8X4),
+                            lhsT_scale=dn_s[:, a, t * P : (t + 1) * P],
+                            rhs=v_w[h][:, a, 2 * c * HCHUNK : 2 * (c + 1) * HCHUNK].bitcast(FP4X4),
+                            rhs_scale=v_s[h][:, a, c * HCHUNK : (c + 1) * HCHUNK],
+                            start=(a == 0),
+                            stop=(a == PASSES - 1),
+                        )
+                nc.scalar.activation(
+                    out=h_bf[h][:, c * HCHUNK : (c + 1) * HCHUNK, :], in_=hs[:].rearrange("p t j -> p j t"), func=ACT.Relu
+                )
+
+        def quantize_hidden(h):
+            nc.vector.quantize_mx(out=h_w[h][:].bitcast(FP8X4), scales=h_s[h][:], in_=h_bf[h][:].rearrange("p j i -> p (j i)"))
+
+        hidden_half(0)
+        gather_words(1)
+        load_x0(54)
+        hidden_half(1)
+
+        wb4_w = held("wb4_w", [P, PASSES, 2 * N], U8)
+        deal(wb4_w[:].bitcast(U16), wb4_raw[:].bitcast(U16), 8)
+        wb8_w = placed("wb8_w", [P, PASSES, N], I32, 2)
+        deal(wb8_w[:], wb8_raw[:], 4)
+        wb4_s = placed("wb4_s", [P, PASSES, N], U8, 0)
+        deal(wb4_s[:], raw_s[1][:], 16)
+        wb8_s = placed("wb8_s", [P, PASSES, N], U8, 1)
+        deal(wb8_s[:], raw_s[2][:], 16)
+
+        up_bf = held("up_bf", [P, N, PACK], BF16)
+        nc.scalar.copy(
+            out=up_bf[:].rearrange("p (t m) i -> p m t i", t=PACK),
+            in_=up_raw[:].rearrange("p i (m t) -> p m t i", t=PACK),
+        )
+        load_x0(22)
+        load_x0(38)
+        quantize_hidden(0)
+        up_w = held("up_w", [P, N], U32)
+        up_s = held("up_s", [P, N], U8)
+        nc.vector.quantize_mx(out=up_w[:].bitcast(FP8X4), scales=up_s[:], in_=up_bf[:].rearrange("p n i -> p (n i)"))
+        quantize_hidden(1)
+
+        b1 = held("b1", [P, PACK], F32)
+        nc.vector.tensor_scalar(out=b1[:], in0=b_raw[:], scalar1=1.0, scalar2=None, op0=ALU.add)
+        y1 = [held("y1_%d" % t, [P, J], F32) for t in range(PACK)]
+        pair = [held("pair%d" % u, [P, 2, J], F32) for u in range(2)]
+        out_bf = [held("out_bf%d" % c, [P, TAIL, PACK], BF16) for c in range(J // TAIL)]
+        out_rows = out_0.rearrange("(p t) j -> p t j", t=PACK)
+
+        def y_tile(t, h):
+            cols = slice(t * P, (t + 1) * P)
+            y = y_psum.tile([P, HALF], F32, name="y")
+            for a in range(PASSES):
+                nc.tensor.matmul_mx(
+                    out=y[:], lhsT=wb4_w[:, a, 2 * t * P : 2 * (t + 1) * P].bitcast(FP4X4), lhsT_scale=wb4_s[:, a, cols],
+                    rhs=v_w[h][:, a, :].bitcast(FP4X4), rhs_scale=v_s[h][:, a, :], start=(a == 0), stop=False,
+                )
+            for a in range(PASSES):
+                nc.tensor.matmul_mx(
+                    out=y[:], lhsT=wb8_w[:, a, cols].bitcast(FP8X4), lhsT_scale=wb8_s[:, a, cols],
+                    rhs=v_w[h][:, a, :].bitcast(FP4X4), rhs_scale=v_s[h][:, a, :], start=False, stop=False,
+                )
+            nc.tensor.matmul_mx(
+                out=y[:], lhsT=up_w[:, cols].bitcast(FP8X4), lhsT_scale=up_s[:, cols],
+                rhs=h_w[h][:].bitcast(FP8X4), rhs_scale=h_s[h][:], start=False, stop=True,
+            )
+            nc.scalar.activation(
+                out=y1[t][:, h * HALF : (h + 1) * HALF], in_=y[:], func=ACT.Identity, bias=b1[:, t : t + 1]
+            )
+
+        def cross(t, j0, n):
+            nc.vector.tensor_tensor(
+                out=pair[t // 2][:, t % 2, j0 : j0 + n], in0=x0[t][:].indirect(listed(j0, n)), in1=y1[t][:, j0 : j0 + n],
+                op=ALU.mult,
+            )
+
+        def round_pair(u, c):
+            nc.scalar.copy(
+                out=out_bf[c][:, :, 2 * u : 2 * u + 2],
+                in_=pair[u][:, :, c * TAIL : (c + 1) * TAIL].rearrange("p e j -> p j e"),
+            )
+
+        for t in range(PACK):
+            for h in range(HALVES):
+                y_tile(t, h)
+        for t in range(PACK - 1):
+            for h in range(HALVES):
+                cross(t, h * HALF, HALF)
+            if t == 1:
+                for c in range(J // TAIL):
+                    round_pair(0, c)
+            nc.sync.dma_start(out=out_rows[:, t, :], in_=pair[t // 2][:, t % 2, :])
+
+        out_w = held("out_w", [P, J], U32)
+        out_s = held("out_s", [P, J], U8)
+        words_out = out_1[0].rearrange("p j f -> p (j f)").bitcast(I32)
+
+        def quantize_out(c):
+            cols = slice(c * TAIL, (c + 1) * TAIL)
+            nc.vector.quantize_mx(
+                out=out_w[:, cols].bitcast(FP8X4), scales=out_s[:, cols], in_=out_bf[c][:].rearrange("p j i -> p (j i)")
+            )
+            if c % 2 == 1:
+                both = slice((c - 1) * TAIL, (c + 1) * TAIL)
+                nc.sync.dma_start(out=words_out[:, both], in_=out_w[:, both].bitcast(I32))
+
+        last = PACK - 1
+        for c in range(J // TAIL):
+            cross(last, c * TAIL, TAIL)
+            round_pair(1, c)
+            if c % 2 == 1:
+                both = slice((c - 1) * TAIL, (c + 1) * TAIL)
+                nc.sync.dma_start(out=out_rows[:, last, both], in_=pair[1][:, 1, both])
+            if c > 0:
+                quantize_out(c - 1)
+        quantize_out(J // TAIL - 1)
+        for q in range(4):
+            queue = nc.sync if q % 2 == 0 else nc.scalar
+            queue.dma_start(out=out_2[0, 4 * q : 4 * q + 4, :].bitcast(I32), in_=out_s[32 * q : 32 * q + 4, :].bitcast(I32))

@@ -43,9 +43,9 @@ def tile_list_xcross_res_reluP_kernel(
         def listed(j0, n):
             return offsets[:, j0 // LIST_ROWS : (j0 + n) // LIST_ROWS]
 
-        def load_scale_rows(queue, plane, scales):
+        def load_scale_rows(plane, scales):
             for q in range(4):
-                queue.dma_start(
+                nc.sync.dma_start(
                     out=plane[32 * q : 32 * q + 4].bitcast(I32),
                     in_=scales[:, 4 * q : 4 * q + 4, :].rearrange("a r c -> r a c").bitcast(I32),
                 )
@@ -59,31 +59,48 @@ def tile_list_xcross_res_reluP_kernel(
         offsets = keep.tile([P, J // LIST_ROWS], U16, name="offsets")
         nc.sync.dma_start(offsets[:], offs)
 
-        def placed(name, shape, dtype, kib):
-            return reuse.tile(shape, dtype, name=name, align_bytes=64, offset=kib * 1024)
+        def placed(name, shape, dtype, half_kib):
+            return reuse.tile(shape, dtype, name=name, align_bytes=64, offset=half_kib * 512)
 
-        def scale_staging(name):
-            tile = held(name, [P, PASSES, N], U8)
-            nc.gpsimd.memset(tile[:].rearrange("p a c -> p (a c)").bitcast(I32), 0)
+        def zeroed(engine, tile):
+            engine.memset(tile[:].rearrange("p a c -> p (a c)").bitcast(I32), 0)
             return tile
 
-        tab_s = placed("tab_s", [P, PASSES, T], U8, 1)
-        nc.vector.memset(tab_s[:].rearrange("p a t -> p (a t)").bitcast(I32), 0)
-        raw_s = []
-        for name, scales in (("dn_raw_s", dn_scales), ("wb4_raw_s", wb4_scales), ("wb8_raw_s", wb8_scales)):
-            raw_s.append(scale_staging(name))
-            load_scale_rows(nc.gpsimd, raw_s[-1], scales)
-        b_raw = held("b_raw", [P, PACK], F32)
+        b_raw = placed("b_raw", [P, PACK], F32, 65)
         nc.scalar.dma_start(out=b_raw[:], in_=b.rearrange("(p t) -> p t", t=PACK))
+        b1 = held("b1", [P, PACK], F32)
+        nc.scalar.activation(out=b1[:], in_=b_raw[:], func=ACT.Copy, bias=1.0)
 
-        dn_raw = placed("dn_raw", [P, PASSES, R], I32, 37)
+        dn_raw = placed("dn_raw", [P, PASSES, R], I32, 40)
         nc.sync.dma_start(out=dn_raw[:], in_=dn_words.rearrange("a p r f -> p a (r f)").bitcast(I32))
-        tab_w = placed("tab_w", [P, T], I32, 54)
+        dn_raw_s = zeroed(nc.gpsimd, placed("dn_raw_s", [P, PASSES, R], U8, 48))
+        load_scale_rows(dn_raw_s, dn_scales)
+        tab_s = zeroed(nc.vector, placed("tab_s", [P, PASSES, T], U8, 97))
+        load_scale_rows(tab_s, tab_scales)
+        tab_w = placed("tab_w", [P, T], I32, 65)
         nc.sync.dma_start(out=tab_w[:], in_=tab_words[0].rearrange("p t f -> p (t f)").bitcast(I32))
-        wb8_raw = held("wb8_raw", [P, PASSES, N], I32)
-        nc.sync.dma_start(out=wb8_raw[:], in_=wb8_words.rearrange("a p n f -> p a (n f)").bitcast(I32))
-        load_scale_rows(nc.scalar, tab_s, tab_scales)
 
+        dn_w = held("dn_w", [P, PASSES, R], I32)
+        deal(dn_w[:], dn_raw[:], 4)
+        dn_s = held("dn_s", [P, PASSES, R], U8)
+        deal(dn_s[:], dn_raw_s[:], 16)
+
+        wb8_raw = placed("wb8_raw", [P, PASSES, N], I32, 33)
+        nc.sync.dma_start(out=wb8_raw[:], in_=wb8_words.rearrange("a p n f -> p a (n f)").bitcast(I32))
+        wb4_raw = placed("wb4_raw", [P, PASSES, 2 * N], U8, 41)
+        nc.sync.dma_start(out=wb4_raw[:].bitcast(I32), in_=wb4_words.rearrange("a p c -> p a c").bitcast(I32))
+        wb4_raw_s = zeroed(nc.gpsimd, placed("wb4_raw_s", [P, PASSES, N], U8, 45))
+        load_scale_rows(wb4_raw_s, wb4_scales)
+        up_raw = placed("up_raw", [P, PACK, N], F32, 49)
+        nc.sync.dma_start(out=up_raw[:], in_=upw.rearrange("(p i) n -> p i n", i=PACK))
+        wb8_raw_s = zeroed(nc.gpsimd, placed("wb8_raw_s", [P, PASSES, N], U8, 47))
+        load_scale_rows(wb8_raw_s, wb8_scales)
+        x0 = []
+
+        def load_x0(half_kib):
+            t = len(x0)
+            x0.append(placed("x0_%d" % t, [P, T], F32, half_kib))
+            nc.sync.dma_start(out=x0[t][:], in_=x0T.rearrange("(p t) c -> p t c", t=PACK)[:, t, :])
 
         v_s, v_w = [], []
 
@@ -94,30 +111,15 @@ def tile_list_xcross_res_reluP_kernel(
             v_s.append(s)
 
         def gather_words(h):
-            both = placed("both", [P, HALF], U32, 0)
+            both = placed("both", [P, HALF], U32, 129)
             nc.vector.tensor_copy(out=both[:], in_=tab_w[:].bitcast(U32).indirect(listed(h * HALF, HALF)))
             w = held("v_w%d" % h, [P, PASSES, 2 * HALF], U8)
             nc.vector.tensor_copy(out=w[:].bitcast(U16), in_=both[:].bitcast(U16).rearrange("p (j a) -> p a j", a=PASSES))
             v_w.append(w)
 
-        dn_w = held("dn_w", [P, PASSES, R], I32)
-        deal(dn_w[:], dn_raw[:], 4)
-        dn_s = held("dn_s", [P, PASSES, R], U8)
-        deal(dn_s[:], raw_s[0][:], 16)
-        wb4_raw = placed("wb4_raw", [P, PASSES, 2 * N], U8, 36)
-        nc.sync.dma_start(out=wb4_raw[:].bitcast(I32), in_=wb4_words.rearrange("a p c -> p a c").bitcast(I32))
-        up_raw = placed("up_raw", [P, PACK, N], F32, 38)
-        nc.sync.dma_start(out=up_raw[:], in_=upw.rearrange("(p i) n -> p i n", i=PACK))
-        x0 = []
-
-        def load_x0(kib):
-            t = len(x0)
-            x0.append(placed("x0_%d" % t, [P, T], F32, kib))
-            nc.sync.dma_start(out=x0[t][:], in_=x0T.rearrange("(p t) c -> p t c", t=PACK)[:, t, :])
-
         for h in range(HALVES):
             gather_scales(h)
-        load_x0(6)
+        load_x0(97)
         gather_words(0)
 
         h_bf = [held("h_bf%d" % h, [P, HALF, PACK], BF16) for h in range(HALVES)]
@@ -147,33 +149,31 @@ def tile_list_xcross_res_reluP_kernel(
 
         hidden_half(0)
         gather_words(1)
-        load_x0(54)
+        load_x0(65)
+        load_x0(129)
         hidden_half(1)
 
+        wb8_w = held("wb8_w", [P, PASSES, N], I32)
+        deal(wb8_w[:], wb8_raw[:], 4)
+        load_x0(2)
         wb4_w = held("wb4_w", [P, PASSES, 2 * N], U8)
         deal(wb4_w[:].bitcast(U16), wb4_raw[:].bitcast(U16), 8)
-        wb8_w = placed("wb8_w", [P, PASSES, N], I32, 2)
-        deal(wb8_w[:], wb8_raw[:], 4)
-        wb4_s = placed("wb4_s", [P, PASSES, N], U8, 0)
-        deal(wb4_s[:], raw_s[1][:], 16)
-        wb8_s = placed("wb8_s", [P, PASSES, N], U8, 1)
-        deal(wb8_s[:], raw_s[2][:], 16)
+        wb4_s = held("wb4_s", [P, PASSES, N], U8)
+        deal(wb4_s[:], wb4_raw_s[:], 16)
+        wb8_s = held("wb8_s", [P, PASSES, N], U8)
+        deal(wb8_s[:], wb8_raw_s[:], 16)
 
         up_bf = held("up_bf", [P, N, PACK], BF16)
         nc.scalar.copy(
             out=up_bf[:].rearrange("p (t m) i -> p m t i", t=PACK),
             in_=up_raw[:].rearrange("p i (m t) -> p m t i", t=PACK),
         )
-        load_x0(22)
-        load_x0(38)
         quantize_hidden(0)
         up_w = held("up_w", [P, N], U32)
         up_s = held("up_s", [P, N], U8)
         nc.vector.quantize_mx(out=up_w[:].bitcast(FP8X4), scales=up_s[:], in_=up_bf[:].rearrange("p n i -> p (n i)"))
         quantize_hidden(1)
 
-        b1 = held("b1", [P, PACK], F32)
-        nc.vector.tensor_scalar(out=b1[:], in0=b_raw[:], scalar1=1.0, scalar2=None, op0=ALU.add)
         y1 = [held("y1_%d" % t, [P, J], F32) for t in range(PACK)]
         pair = [held("pair%d" % u, [P, 2, J], F32) for u in range(2)]
         out_bf = [held("out_bf%d" % c, [P, TAIL, PACK], BF16) for c in range(J // TAIL)]

@@ -22,8 +22,9 @@ PASSES = K // (P * PACK)
 HALF = 512
 HALVES = J // HALF
 HCHUNK = 128
-TAIL = 256
+CHUNKS = (slice(0, 256), slice(256, 512), slice(512, 768), slice(768, 896), slice(896, 1024))
 LIST_ROWS = 16
+UP_PIECES = 4
 
 
 def tile_list_xcross_res_reluP_kernel(
@@ -34,20 +35,24 @@ def tile_list_xcross_res_reluP_kernel(
     with ExitStack() as ctx:
         keep = ctx.enter_context(tc.tile_pool(name="keep", bufs=1))
         reuse = ctx.enter_context(tc.tile_pool(name="reuse", bufs=1))
+        picks = ctx.enter_context(tc.tile_pool(name="picks", bufs=4))
         hs_psum = ctx.enter_context(tc.psum_pool(name="hs_psum", bufs=3))
         y_psum = ctx.enter_context(tc.psum_pool(name="y_psum", bufs=5))
 
         def held(name, shape, dtype):
             return keep.tile(shape, dtype, name=name, align_bytes=64)
 
+        def placed(name, shape, dtype, unit):
+            return reuse.tile(shape, dtype, name=name, align_bytes=64, offset=unit * 512)
+
         def listed(j0, n):
             return offsets[:, j0 // LIST_ROWS : (j0 + n) // LIST_ROWS]
 
         def load_scale_rows(plane, scales):
-            for q in range(4):
+            for r in range(4):
                 nc.sync.dma_start(
-                    out=plane[32 * q : 32 * q + 4].bitcast(I32),
-                    in_=scales[:, 4 * q : 4 * q + 4, :].rearrange("a r c -> r a c").bitcast(I32),
+                    out=plane[r:P:32].bitcast(I32),
+                    in_=scales.rearrange("a (q r) c -> r q a c", r=4)[r].bitcast(I32),
                 )
 
         def deal(out, in_, run):
@@ -56,71 +61,81 @@ def tile_list_xcross_res_reluP_kernel(
                 in_=in_.rearrange("p a (c i t) -> p a c t i", t=PACK, i=run),
             )
 
+        def zero_planes(engine, tile):
+            engine.memset(tile[:].rearrange("p a c -> p (a c)").bitcast(I32), 0)
+
         offsets = keep.tile([P, J // LIST_ROWS], U16, name="offsets")
         nc.sync.dma_start(offsets[:], offs)
 
-        def placed(name, shape, dtype, half_kib):
-            return reuse.tile(shape, dtype, name=name, align_bytes=64, offset=half_kib * 512)
-
-        def zeroed(engine, tile):
-            engine.memset(tile[:].rearrange("p a c -> p (a c)").bitcast(I32), 0)
-            return tile
-
-        b_raw = placed("b_raw", [P, PACK], F32, 65)
+        b_raw = placed("b_raw", [P, PACK], F32, 62)
         nc.scalar.dma_start(out=b_raw[:], in_=b.rearrange("(p t) -> p t", t=PACK))
         b1 = held("b1", [P, PACK], F32)
         nc.scalar.activation(out=b1[:], in_=b_raw[:], func=ACT.Copy, bias=1.0)
 
-        dn_raw = placed("dn_raw", [P, PASSES, R], I32, 40)
+        dn_raw = held("dn_raw", [P, PASSES, R], I32)
         nc.sync.dma_start(out=dn_raw[:], in_=dn_words.rearrange("a p r f -> p a (r f)").bitcast(I32))
-        dn_raw_s = zeroed(nc.gpsimd, placed("dn_raw_s", [P, PASSES, R], U8, 48))
+        wb8_raw = held("wb8_raw", [P, PASSES, N], I32)
+        nc.sync.dma_start(out=wb8_raw[:], in_=wb8_words.rearrange("a p n f -> p a (n f)").bitcast(I32))
+        wb4_raw = held("wb4_raw", [P, PASSES, 2 * N], U8)
+        nc.sync.dma_start(out=wb4_raw[:].bitcast(I32), in_=wb4_words.rearrange("a p c -> p a c").bitcast(I32))
+        dn_raw_s = placed("dn_raw_s", [P, PASSES, R], U8, 95)
+        zero_planes(nc.gpsimd, dn_raw_s)
         load_scale_rows(dn_raw_s, dn_scales)
-        tab_s = zeroed(nc.vector, placed("tab_s", [P, PASSES, T], U8, 97))
-        load_scale_rows(tab_s, tab_scales)
-        tab_w = placed("tab_w", [P, T], I32, 65)
+        tab_s = placed("tab_s", [P, T], U8, 24)
+        nc.vector.memset(tab_s[:].bitcast(I32), 0)
+        nc.sync.dma_start(out=tab_s[0:P:4, :].bitcast(I32), in_=tab_scales.rearrange("a q t -> (a q) t").bitcast(I32))
+        tab_w = placed("tab_w", [P, T], I32, 62)
         nc.sync.dma_start(out=tab_w[:], in_=tab_words[0].rearrange("p t f -> p (t f)").bitcast(I32))
+        v_s = held("v_s", [P, PASSES, J], U8)
+        zero_planes(nc.gpsimd, v_s)
 
+        picked_s = held("picked_s", [P, J], U8)
+        nc.vector.tensor_copy(out=picked_s[:], in_=tab_s[:].indirect(offsets[:]))
         dn_w = held("dn_w", [P, PASSES, R], I32)
         deal(dn_w[:], dn_raw[:], 4)
-        dn_s = held("dn_s", [P, PASSES, R], U8)
+        wb8_w = held("wb8_w", [P, PASSES, N], I32)
+        deal(wb8_w[:], wb8_raw[:], 4)
+        wb4_w = held("wb4_w", [P, PASSES, 2 * N], U8)
+        deal(wb4_w[:].bitcast(U16), wb4_raw[:].bitcast(U16), 8)
+
+        def move_scale_rows(a, r):
+            nc.sync.dma_start(
+                out=v_s[r:P:32, a, :].bitcast(I32), in_=picked_s[64 * a + 4 * r : 64 * (a + 1) : 16, :].bitcast(I32)
+            )
+
+        moves = [(a, r) for a in range(PASSES) for r in range(4)]
+        for a, r in moves[:6]:
+            move_scale_rows(a, r)
+        up_raw = placed("up_raw", [P, PACK, N], F32, 30)
+        nc.sync.dma_start(out=up_raw[:], in_=upw.rearrange("(p i) n -> p i n", i=PACK))
+        for a, r in moves[6:]:
+            move_scale_rows(a, r)
+        wb8_raw_s = placed("wb8_raw_s", [P, PASSES, N], U8, 24)
+        zero_planes(nc.vector, wb8_raw_s)
+        load_scale_rows(wb8_raw_s, wb8_scales)
+        dn_s = placed("dn_s", [P, PASSES, R], U8, 26)
         deal(dn_s[:], dn_raw_s[:], 16)
 
-        wb8_raw = placed("wb8_raw", [P, PASSES, N], I32, 33)
-        nc.sync.dma_start(out=wb8_raw[:], in_=wb8_words.rearrange("a p n f -> p a (n f)").bitcast(I32))
-        wb4_raw = placed("wb4_raw", [P, PASSES, 2 * N], U8, 41)
-        nc.sync.dma_start(out=wb4_raw[:].bitcast(I32), in_=wb4_words.rearrange("a p c -> p a c").bitcast(I32))
-        wb4_raw_s = zeroed(nc.gpsimd, placed("wb4_raw_s", [P, PASSES, N], U8, 45))
-        load_scale_rows(wb4_raw_s, wb4_scales)
-        up_raw = placed("up_raw", [P, PACK, N], F32, 49)
-        nc.sync.dma_start(out=up_raw[:], in_=upw.rearrange("(p i) n -> p i n", i=PACK))
-        wb8_raw_s = zeroed(nc.gpsimd, placed("wb8_raw_s", [P, PASSES, N], U8, 47))
-        load_scale_rows(wb8_raw_s, wb8_scales)
         x0 = []
 
-        def load_x0(half_kib):
+        def load_x0(unit):
             t = len(x0)
-            x0.append(placed("x0_%d" % t, [P, T], F32, half_kib))
+            x0.append(placed("x0_%d" % t, [P, T], F32, unit))
             nc.sync.dma_start(out=x0[t][:], in_=x0T.rearrange("(p t) c -> p t c", t=PACK)[:, t, :])
 
-        v_s, v_w = [], []
+        load_x0(96)
+        wb4_raw_s = placed("wb4_raw_s", [P, PASSES, N], U8, 94)
+        zero_planes(nc.vector, wb4_raw_s)
+        load_scale_rows(wb4_raw_s, wb4_scales)
 
-        def gather_scales(h):
-            s = held("v_s%d" % h, [P, PASSES, HALF], U8)
-            for a in range(PASSES):
-                nc.vector.tensor_copy(out=s[:, a, :], in_=tab_s[:, a, :].indirect(listed(h * HALF, HALF)))
-            v_s.append(s)
+        v_w = []
 
         def gather_words(h):
-            both = placed("both", [P, HALF], U32, 129)
+            both = placed("both", [P, HALF], U32, 128)
             nc.vector.tensor_copy(out=both[:], in_=tab_w[:].bitcast(U32).indirect(listed(h * HALF, HALF)))
             w = held("v_w%d" % h, [P, PASSES, 2 * HALF], U8)
             nc.vector.tensor_copy(out=w[:].bitcast(U16), in_=both[:].bitcast(U16).rearrange("p (j a) -> p a j", a=PASSES))
             v_w.append(w)
-
-        for h in range(HALVES):
-            gather_scales(h)
-        load_x0(97)
-        gather_words(0)
 
         h_bf = [held("h_bf%d" % h, [P, HALF, PACK], BF16) for h in range(HALVES)]
         h_w = [held("h_w%d" % h, [P, HALF], U32) for h in range(HALVES)]
@@ -129,6 +144,7 @@ def tile_list_xcross_res_reluP_kernel(
         def hidden_half(h):
             for c in range(HALF // HCHUNK):
                 hs = hs_psum.tile([P, PACK, HCHUNK], F32, name="hs")
+                j0 = h * HALF + c * HCHUNK
                 for t in range(PACK):
                     for a in range(PASSES):
                         nc.tensor.matmul_mx(
@@ -136,7 +152,7 @@ def tile_list_xcross_res_reluP_kernel(
                             lhsT=dn_w[:, a, t * P : (t + 1) * P].bitcast(FP8X4),
                             lhsT_scale=dn_s[:, a, t * P : (t + 1) * P],
                             rhs=v_w[h][:, a, 2 * c * HCHUNK : 2 * (c + 1) * HCHUNK].bitcast(FP4X4),
-                            rhs_scale=v_s[h][:, a, c * HCHUNK : (c + 1) * HCHUNK],
+                            rhs_scale=v_s[:, a, j0 : j0 + HCHUNK],
                             start=(a == 0),
                             stop=(a == PASSES - 1),
                         )
@@ -147,105 +163,108 @@ def tile_list_xcross_res_reluP_kernel(
         def quantize_hidden(h):
             nc.vector.quantize_mx(out=h_w[h][:].bitcast(FP8X4), scales=h_s[h][:], in_=h_bf[h][:].rearrange("p j i -> p (j i)"))
 
+        gather_words(0)
         hidden_half(0)
         gather_words(1)
-        load_x0(65)
-        load_x0(129)
+        load_x0(62)
+        load_x0(128)
         hidden_half(1)
 
-        wb8_w = held("wb8_w", [P, PASSES, N], I32)
-        deal(wb8_w[:], wb8_raw[:], 4)
-        load_x0(2)
-        wb4_w = held("wb4_w", [P, PASSES, 2 * N], U8)
-        deal(wb4_w[:].bitcast(U16), wb4_raw[:].bitcast(U16), 8)
-        wb4_s = held("wb4_s", [P, PASSES, N], U8)
-        deal(wb4_s[:], wb4_raw_s[:], 16)
         wb8_s = held("wb8_s", [P, PASSES, N], U8)
         deal(wb8_s[:], wb8_raw_s[:], 16)
 
         up_bf = held("up_bf", [P, N, PACK], BF16)
-        nc.scalar.copy(
-            out=up_bf[:].rearrange("p (t m) i -> p m t i", t=PACK),
-            in_=up_raw[:].rearrange("p i (m t) -> p m t i", t=PACK),
-        )
+        for piece in range(UP_PIECES):
+            ms = slice(piece * P // UP_PIECES, (piece + 1) * P // UP_PIECES)
+            nc.scalar.copy(
+                out=up_bf[:].rearrange("p (t m) i -> p m t i", t=PACK)[:, ms],
+                in_=up_raw[:].rearrange("p i (m t) -> p m t i", t=PACK)[:, ms],
+            )
+        load_x0(30)
         quantize_hidden(0)
         up_w = held("up_w", [P, N], U32)
         up_s = held("up_s", [P, N], U8)
         nc.vector.quantize_mx(out=up_w[:].bitcast(FP8X4), scales=up_s[:], in_=up_bf[:].rearrange("p n i -> p (n i)"))
         quantize_hidden(1)
+        wb4_s = held("wb4_s", [P, PASSES, N], U8)
+        deal(wb4_s[:], wb4_raw_s[:], 16)
 
-        y1 = [held("y1_%d" % t, [P, J], F32) for t in range(PACK)]
         pair = [held("pair%d" % u, [P, 2, J], F32) for u in range(2)]
-        out_bf = [held("out_bf%d" % c, [P, TAIL, PACK], BF16) for c in range(J // TAIL)]
+        out_bf = [held("out_bf%d" % c, [P, js.stop - js.start, PACK], BF16) for c, js in enumerate(CHUNKS)]
         out_rows = out_0.rearrange("(p t) j -> p t j", t=PACK)
 
-        def y_tile(t, h):
+        def y_sum(t, h):
             cols = slice(t * P, (t + 1) * P)
+            js = slice(h * HALF, (h + 1) * HALF)
             y = y_psum.tile([P, HALF], F32, name="y")
             for a in range(PASSES):
                 nc.tensor.matmul_mx(
-                    out=y[:], lhsT=wb4_w[:, a, 2 * t * P : 2 * (t + 1) * P].bitcast(FP4X4), lhsT_scale=wb4_s[:, a, cols],
-                    rhs=v_w[h][:, a, :].bitcast(FP4X4), rhs_scale=v_s[h][:, a, :], start=(a == 0), stop=False,
-                )
-            for a in range(PASSES):
-                nc.tensor.matmul_mx(
                     out=y[:], lhsT=wb8_w[:, a, cols].bitcast(FP8X4), lhsT_scale=wb8_s[:, a, cols],
-                    rhs=v_w[h][:, a, :].bitcast(FP4X4), rhs_scale=v_s[h][:, a, :], start=False, stop=False,
+                    rhs=v_w[h][:, a, :].bitcast(FP4X4), rhs_scale=v_s[:, a, js], start=(a == 0), stop=False,
                 )
             nc.tensor.matmul_mx(
                 out=y[:], lhsT=up_w[:, cols].bitcast(FP8X4), lhsT_scale=up_s[:, cols],
-                rhs=h_w[h][:].bitcast(FP8X4), rhs_scale=h_s[h][:], start=False, stop=True,
+                rhs=h_w[h][:].bitcast(FP8X4), rhs_scale=h_s[h][:], start=False, stop=False,
             )
-            nc.scalar.activation(
-                out=y1[t][:, h * HALF : (h + 1) * HALF], in_=y[:], func=ACT.Identity, bias=b1[:, t : t + 1]
-            )
-
-        def cross(t, j0, n):
-            nc.vector.tensor_tensor(
-                out=pair[t // 2][:, t % 2, j0 : j0 + n], in0=x0[t][:].indirect(listed(j0, n)), in1=y1[t][:, j0 : j0 + n],
-                op=ALU.mult,
-            )
+            for a in range(PASSES):
+                nc.tensor.matmul_mx(
+                    out=y[:], lhsT=wb4_w[:, a, 2 * t * P : 2 * (t + 1) * P].bitcast(FP4X4), lhsT_scale=wb4_s[:, a, cols],
+                    rhs=v_w[h][:, a, :].bitcast(FP4X4), rhs_scale=v_s[:, a, js], start=False, stop=(a == PASSES - 1),
+                )
+            return y
 
         def round_pair(u, c):
             nc.scalar.copy(
                 out=out_bf[c][:, :, 2 * u : 2 * u + 2],
-                in_=pair[u][:, :, c * TAIL : (c + 1) * TAIL].rearrange("p e j -> p j e"),
+                in_=pair[u][:, :, CHUNKS[c]].rearrange("p e j -> p j e"),
             )
 
-        for t in range(PACK):
+        last = PACK - 1
+        y_last = held("y_last", [P, J], F32)
+
+        def cross(t, h):
+            js = slice(h * HALF, (h + 1) * HALF)
+            y = y_sum(t, h)
+            picked = picks.tile([P, HALF], F32, name="picked")
+            nc.vector.tensor_copy(out=picked[:], in_=x0[t][:].indirect(listed(h * HALF, HALF)))
+            nc.vector.scalar_tensor_tensor(
+                out=pair[t // 2][:, t % 2, js], in0=y[:], scalar=b1[:, t : t + 1], in1=picked[:], op0=ALU.add, op1=ALU.mult
+            )
+
+        for t in range(2):
             for h in range(HALVES):
-                y_tile(t, h)
-        for t in range(PACK - 1):
-            for h in range(HALVES):
-                cross(t, h * HALF, HALF)
-            if t == 1:
-                for c in range(J // TAIL):
-                    round_pair(0, c)
-            nc.sync.dma_start(out=out_rows[:, t, :], in_=pair[t // 2][:, t % 2, :])
+                cross(t, h)
+            nc.sync.dma_start(out=out_rows[:, t, :], in_=pair[0][:, t, :])
+        for c in range(len(CHUNKS)):
+            round_pair(0, c)
+        cross(2, 0)
+        for h in range(HALVES):
+            nc.scalar.activation(
+                out=y_last[:, h * HALF : (h + 1) * HALF], in_=y_sum(last, h)[:], func=ACT.Identity, bias=b1[:, last : last + 1]
+            )
+        cross(2, 1)
+        nc.sync.dma_start(out=out_rows[:, 2, :], in_=pair[1][:, 0, :])
 
         out_w = held("out_w", [P, J], U32)
         out_s = held("out_s", [P, J], U8)
         words_out = out_1[0].rearrange("p j f -> p (j f)").bitcast(I32)
 
-        def quantize_out(c):
-            cols = slice(c * TAIL, (c + 1) * TAIL)
-            nc.vector.quantize_mx(
-                out=out_w[:, cols].bitcast(FP8X4), scales=out_s[:, cols], in_=out_bf[c][:].rearrange("p j i -> p (j i)")
+        for c, js in enumerate(CHUNKS):
+            nc.vector.tensor_tensor(
+                out=pair[1][:, 1, js], in0=x0[last][:].indirect(listed(js.start, js.stop - js.start)), in1=y_last[:, js],
+                op=ALU.mult,
             )
-            if c % 2 == 1:
-                both = slice((c - 1) * TAIL, (c + 1) * TAIL)
-                nc.sync.dma_start(out=words_out[:, both], in_=out_w[:, both].bitcast(I32))
-
-        last = PACK - 1
-        for c in range(J // TAIL):
-            cross(last, c * TAIL, TAIL)
             round_pair(1, c)
-            if c % 2 == 1:
-                both = slice((c - 1) * TAIL, (c + 1) * TAIL)
-                nc.sync.dma_start(out=out_rows[:, last, both], in_=pair[1][:, 1, both])
-            if c > 0:
-                quantize_out(c - 1)
-        quantize_out(J // TAIL - 1)
-        for q in range(4):
-            queue = nc.sync if q % 2 == 0 else nc.scalar
-            queue.dma_start(out=out_2[0, 4 * q : 4 * q + 4, :].bitcast(I32), in_=out_s[32 * q : 32 * q + 4, :].bitcast(I32))
+            if js.stop % HALF == 0:
+                half = slice(js.stop - HALF, js.stop)
+                nc.sync.dma_start(out=out_rows[:, last, half], in_=pair[1][:, 1, half])
+        for c, js in enumerate(CHUNKS):
+            nc.vector.quantize_mx(
+                out=out_w[:, js].bitcast(FP8X4), scales=out_s[:, js], in_=out_bf[c][:].rearrange("p j i -> p (j i)")
+            )
+            if js.stop % HALF == 0:
+                half = slice(js.stop - HALF, js.stop)
+                nc.sync.dma_start(out=words_out[:, half], in_=out_w[:, half].bitcast(I32))
+        for r in range(4):
+            queue = nc.sync if r % 2 == 0 else nc.scalar
+            queue.dma_start(out=out_2[0, r::4, :].bitcast(I32), in_=out_s[r:P:32, :].bitcast(I32))

@@ -24,7 +24,7 @@ HALVES = J // HALF
 HCHUNK = 128
 CHUNKS = (slice(0, 256), slice(256, 512), slice(512, 768), slice(768, 896), slice(896, 1024))
 LIST_ROWS = 16
-UP_PIECES = 4
+UP_PIECES = 1
 
 
 def tile_list_xcross_res_reluP_kernel(
@@ -35,9 +35,7 @@ def tile_list_xcross_res_reluP_kernel(
     with ExitStack() as ctx:
         keep = ctx.enter_context(tc.tile_pool(name="keep", bufs=1))
         reuse = ctx.enter_context(tc.tile_pool(name="reuse", bufs=1))
-        picks = ctx.enter_context(tc.tile_pool(name="picks", bufs=4))
-        hs_psum = ctx.enter_context(tc.psum_pool(name="hs_psum", bufs=3))
-        y_psum = ctx.enter_context(tc.psum_pool(name="y_psum", bufs=5))
+        psum = ctx.enter_context(tc.psum_pool(name="psum", bufs=8))
 
         def held(name, shape, dtype):
             return keep.tile(shape, dtype, name=name, align_bytes=64)
@@ -48,9 +46,9 @@ def tile_list_xcross_res_reluP_kernel(
         def listed(j0, n):
             return offsets[:, j0 // LIST_ROWS : (j0 + n) // LIST_ROWS]
 
-        def load_scale_rows(plane, scales):
+        def load_scale_rows(queue, plane, scales):
             for r in range(4):
-                nc.sync.dma_start(
+                queue.dma_start(
                     out=plane[r:P:32].bitcast(I32),
                     in_=scales.rearrange("a (q r) c -> r q a c", r=4)[r].bitcast(I32),
                 )
@@ -67,36 +65,38 @@ def tile_list_xcross_res_reluP_kernel(
         offsets = keep.tile([P, J // LIST_ROWS], U16, name="offsets")
         nc.sync.dma_start(offsets[:], offs)
 
-        b_raw = placed("b_raw", [P, PACK], F32, 62)
-        nc.scalar.dma_start(out=b_raw[:], in_=b.rearrange("(p t) -> p t", t=PACK))
+        b_raw = reuse.tile([P, 32], F32, name="b_raw", align_bytes=64, offset=40 * 512 - 64)
+        nc.sync.dma_start(out=b_raw[:, 0:PACK], in_=b.rearrange("(p t) -> p t", t=PACK))
         b1 = held("b1", [P, PACK], F32)
-        nc.scalar.activation(out=b1[:], in_=b_raw[:], func=ACT.Copy, bias=1.0)
+        nc.vector.tensor_scalar_add(out=b1[:], in0=b_raw[:, 0:PACK], scalar1=1.0)
 
         dn_raw = held("dn_raw", [P, PASSES, R], I32)
         nc.sync.dma_start(out=dn_raw[:], in_=dn_words.rearrange("a p r f -> p a (r f)").bitcast(I32))
         wb8_raw = held("wb8_raw", [P, PASSES, N], I32)
         nc.sync.dma_start(out=wb8_raw[:], in_=wb8_words.rearrange("a p n f -> p a (n f)").bitcast(I32))
-        wb4_raw = held("wb4_raw", [P, PASSES, 2 * N], U8)
-        nc.sync.dma_start(out=wb4_raw[:].bitcast(I32), in_=wb4_words.rearrange("a p c -> p a c").bitcast(I32))
-        dn_raw_s = placed("dn_raw_s", [P, PASSES, R], U8, 95)
-        zero_planes(nc.gpsimd, dn_raw_s)
-        load_scale_rows(dn_raw_s, dn_scales)
-        tab_s = placed("tab_s", [P, T], U8, 24)
+        tab_s = placed("tab_s", [P, T], U8, 187)
         nc.vector.memset(tab_s[:].bitcast(I32), 0)
         nc.sync.dma_start(out=tab_s[0:P:4, :].bitcast(I32), in_=tab_scales.rearrange("a q t -> (a q) t").bitcast(I32))
-        tab_w = placed("tab_w", [P, T], I32, 62)
-        nc.sync.dma_start(out=tab_w[:], in_=tab_words[0].rearrange("p t f -> p (t f)").bitcast(I32))
+        dn_raw_s = placed("dn_raw_s", [P, PASSES, R], U8, 103)
+        zero_planes(nc.vector, dn_raw_s)
+        load_scale_rows(nc.sync, dn_raw_s, dn_scales)
+        wb8_raw_s = held("wb8_raw_s", [P, PASSES, N], U8)
+        zero_planes(nc.gpsimd, wb8_raw_s)
+        wb4_raw_s = held("wb4_raw_s", [P, PASSES, N], U8)
+        zero_planes(nc.gpsimd, wb4_raw_s)
+        load_scale_rows(nc.gpsimd, wb8_raw_s, wb8_scales)
+        load_scale_rows(nc.gpsimd, wb4_raw_s, wb4_scales)
         v_s = held("v_s", [P, PASSES, J], U8)
-        zero_planes(nc.gpsimd, v_s)
+        zero_planes(nc.vector, v_s)
+        wb4_raw = placed("wb4_raw", [P, PASSES, 2 * N], U8, 36)
+        nc.sync.dma_start(out=wb4_raw[:].bitcast(I32), in_=wb4_words.rearrange("a p c -> p a c").bitcast(I32))
+        tab_w = placed("tab_w", [P, T], I32, 40)
+        nc.sync.dma_start(out=tab_w[:], in_=tab_words[0].rearrange("p t f -> p (t f)").bitcast(I32))
 
         picked_s = held("picked_s", [P, J], U8)
         nc.vector.tensor_copy(out=picked_s[:], in_=tab_s[:].indirect(offsets[:]))
         dn_w = held("dn_w", [P, PASSES, R], I32)
         deal(dn_w[:], dn_raw[:], 4)
-        wb8_w = held("wb8_w", [P, PASSES, N], I32)
-        deal(wb8_w[:], wb8_raw[:], 4)
-        wb4_w = held("wb4_w", [P, PASSES, 2 * N], U8)
-        deal(wb4_w[:].bitcast(U16), wb4_raw[:].bitcast(U16), 8)
 
         def move_scale_rows(a, r):
             nc.sync.dma_start(
@@ -106,15 +106,16 @@ def tile_list_xcross_res_reluP_kernel(
         moves = [(a, r) for a in range(PASSES) for r in range(4)]
         for a, r in moves[:6]:
             move_scale_rows(a, r)
-        up_raw = placed("up_raw", [P, PACK, N], F32, 30)
+        up_raw = placed("up_raw", [P, PACK, N], F32, 172)
         nc.sync.dma_start(out=up_raw[:], in_=upw.rearrange("(p i) n -> p i n", i=PACK))
         for a, r in moves[6:]:
             move_scale_rows(a, r)
-        wb8_raw_s = placed("wb8_raw_s", [P, PASSES, N], U8, 24)
-        zero_planes(nc.vector, wb8_raw_s)
-        load_scale_rows(wb8_raw_s, wb8_scales)
-        dn_s = placed("dn_s", [P, PASSES, R], U8, 26)
+        dn_s = placed("dn_s", [P, PASSES, R], U8, 189)
         deal(dn_s[:], dn_raw_s[:], 16)
+        wb4_w = placed("wb4_w", [P, PASSES, 2 * N], U8, 194)
+        deal(wb4_w[:].bitcast(U16), wb4_raw[:].bitcast(U16), 8)
+        wb8_w = placed("wb8_w", [P, PASSES, N], I32, 96)
+        deal(wb8_w[:], wb8_raw[:], 4)
 
         x0 = []
 
@@ -123,38 +124,36 @@ def tile_list_xcross_res_reluP_kernel(
             x0.append(placed("x0_%d" % t, [P, T], F32, unit))
             nc.sync.dma_start(out=x0[t][:], in_=x0T.rearrange("(p t) c -> p t c", t=PACK)[:, t, :])
 
-        load_x0(96)
-        wb4_raw_s = placed("wb4_raw_s", [P, PASSES, N], U8, 94)
-        zero_planes(nc.vector, wb4_raw_s)
-        load_scale_rows(wb4_raw_s, wb4_scales)
+        load_x0(104)
 
         v_w = []
 
+
         def gather_words(h):
-            both = placed("both", [P, HALF], U32, 128)
+            both = placed("both", [P, HALF], U32, 137)
             nc.vector.tensor_copy(out=both[:], in_=tab_w[:].bitcast(U32).indirect(listed(h * HALF, HALF)))
             w = held("v_w%d" % h, [P, PASSES, 2 * HALF], U8)
             nc.vector.tensor_copy(out=w[:].bitcast(U16), in_=both[:].bitcast(U16).rearrange("p (j a) -> p a j", a=PASSES))
             v_w.append(w)
 
-        h_bf = [held("h_bf%d" % h, [P, HALF, PACK], BF16) for h in range(HALVES)]
+        h_bf = [placed("h_bf%d" % h, [P, HALF, PACK], BF16, (1, 206)[h]) for h in range(HALVES)]
         h_w = [held("h_w%d" % h, [P, HALF], U32) for h in range(HALVES)]
         h_s = [held("h_s%d" % h, [P, HALF], U8) for h in range(HALVES)]
 
         def hidden_half(h):
             for c in range(HALF // HCHUNK):
-                hs = hs_psum.tile([P, PACK, HCHUNK], F32, name="hs")
+                hs = psum.tile([P, PACK, HCHUNK], F32, name="hs", tag="bank")
                 j0 = h * HALF + c * HCHUNK
                 for t in range(PACK):
-                    for a in range(PASSES):
+                    for a in reversed(range(PASSES)):
                         nc.tensor.matmul_mx(
                             out=hs[:, t, :],
                             lhsT=dn_w[:, a, t * P : (t + 1) * P].bitcast(FP8X4),
                             lhsT_scale=dn_s[:, a, t * P : (t + 1) * P],
                             rhs=v_w[h][:, a, 2 * c * HCHUNK : 2 * (c + 1) * HCHUNK].bitcast(FP4X4),
                             rhs_scale=v_s[:, a, j0 : j0 + HCHUNK],
-                            start=(a == 0),
-                            stop=(a == PASSES - 1),
+                            start=(a == PASSES - 1),
+                            stop=(a == 0),
                         )
                 nc.scalar.activation(
                     out=h_bf[h][:, c * HCHUNK : (c + 1) * HCHUNK, :], in_=hs[:].rearrange("p t j -> p j t"), func=ACT.Relu
@@ -163,30 +162,30 @@ def tile_list_xcross_res_reluP_kernel(
         def quantize_hidden(h):
             nc.vector.quantize_mx(out=h_w[h][:].bitcast(FP8X4), scales=h_s[h][:], in_=h_bf[h][:].rearrange("p j i -> p (j i)"))
 
-        gather_words(0)
-        hidden_half(0)
-        gather_words(1)
-        load_x0(62)
-        load_x0(128)
-        hidden_half(1)
-
-        wb8_s = held("wb8_s", [P, PASSES, N], U8)
-        deal(wb8_s[:], wb8_raw_s[:], 16)
-
         up_bf = held("up_bf", [P, N, PACK], BF16)
         for piece in range(UP_PIECES):
             ms = slice(piece * P // UP_PIECES, (piece + 1) * P // UP_PIECES)
-            nc.scalar.copy(
+            nc.gpsimd.tensor_scalar(
                 out=up_bf[:].rearrange("p (t m) i -> p m t i", t=PACK)[:, ms],
-                in_=up_raw[:].rearrange("p i (m t) -> p m t i", t=PACK)[:, ms],
+                in0=up_raw[:].rearrange("p i (m t) -> p m t i", t=PACK)[:, ms],
+                scalar1=1.0, scalar2=0.0, op0=ALU.mult, op1=ALU.add,
             )
-        load_x0(30)
+        gather_words(0)
+        hidden_half(0)
+        gather_words(1)
+        load_x0(16)
+        load_x0(64)
+        load_x0(140)
+        hidden_half(1)
+
+        wb8_s = placed("wb8_s", [P, PASSES, N], U8, 136)
+        deal(wb8_s[:], wb8_raw_s[:], 16)
+
         quantize_hidden(0)
         up_w = held("up_w", [P, N], U32)
         up_s = held("up_s", [P, N], U8)
         nc.vector.quantize_mx(out=up_w[:].bitcast(FP8X4), scales=up_s[:], in_=up_bf[:].rearrange("p n i -> p (n i)"))
-        quantize_hidden(1)
-        wb4_s = held("wb4_s", [P, PASSES, N], U8)
+        wb4_s = placed("wb4_s", [P, PASSES, N], U8, 0)
         deal(wb4_s[:], wb4_raw_s[:], 16)
 
         pair = [held("pair%d" % u, [P, 2, J], F32) for u in range(2)]
@@ -196,7 +195,7 @@ def tile_list_xcross_res_reluP_kernel(
         def y_sum(t, h):
             cols = slice(t * P, (t + 1) * P)
             js = slice(h * HALF, (h + 1) * HALF)
-            y = y_psum.tile([P, HALF], F32, name="y")
+            y = psum.tile([P, HALF], F32, name="y", tag="bank")
             for a in range(PASSES):
                 nc.tensor.matmul_mx(
                     out=y[:], lhsT=wb8_w[:, a, cols].bitcast(FP8X4), lhsT_scale=wb8_s[:, a, cols],
@@ -222,27 +221,34 @@ def tile_list_xcross_res_reluP_kernel(
         last = PACK - 1
         y_last = held("y_last", [P, J], F32)
 
-        def cross(t, h):
-            js = slice(h * HALF, (h + 1) * HALF)
-            y = y_sum(t, h)
-            picked = picks.tile([P, HALF], F32, name="picked")
-            nc.vector.tensor_copy(out=picked[:], in_=x0[t][:].indirect(listed(h * HALF, HALF)))
-            nc.vector.scalar_tensor_tensor(
-                out=pair[t // 2][:, t % 2, js], in0=y[:], scalar=b1[:, t : t + 1], in1=picked[:], op0=ALU.add, op1=ALU.mult
-            )
-
-        for t in range(2):
+        def pick(t):
+            picked = placed("picked%d" % t, [P, J], F32, (2, 206, 198)[t])
             for h in range(HALVES):
-                cross(t, h)
+                nc.vector.tensor_copy(
+                    out=picked[:, h * HALF : (h + 1) * HALF], in_=x0[t][:].indirect(listed(h * HALF, HALF))
+                )
+            return picked
+
+        def cross(t, picked):
+            for h in range(HALVES):
+                js = slice(h * HALF, (h + 1) * HALF)
+                nc.vector.scalar_tensor_tensor(
+                    out=pair[t // 2][:, t % 2, js], in0=y_sum(t, h)[:], scalar=b1[:, t : t + 1], in1=picked[:, js],
+                    op0=ALU.add, op1=ALU.mult,
+                )
+
+        first = pick(0)
+        quantize_hidden(1)
+        for t in range(2):
+            cross(t, first if t == 0 else pick(t))
             nc.sync.dma_start(out=out_rows[:, t, :], in_=pair[0][:, t, :])
         for c in range(len(CHUNKS)):
             round_pair(0, c)
-        cross(2, 0)
+        cross(2, pick(2))
         for h in range(HALVES):
             nc.scalar.activation(
                 out=y_last[:, h * HALF : (h + 1) * HALF], in_=y_sum(last, h)[:], func=ACT.Identity, bias=b1[:, last : last + 1]
             )
-        cross(2, 1)
         nc.sync.dma_start(out=out_rows[:, 2, :], in_=pair[1][:, 0, :])
 
         out_w = held("out_w", [P, J], U32)

@@ -23,6 +23,7 @@ HALF = 512
 HALVES = J // HALF
 HCHUNK = 128
 CHUNKS = (slice(0, 256), slice(256, 512), slice(512, 768), slice(768, 896), slice(896, 1024))
+STORED = {512: slice(0, 512), 896: slice(512, 896), 1024: slice(896, 1024)}
 LIST_ROWS = 16
 UP_PIECES = 1
 
@@ -104,11 +105,11 @@ def tile_list_xcross_res_reluP_kernel(
             )
 
         moves = [(a, r) for a in range(PASSES) for r in range(4)]
-        for a, r in moves[:6]:
+        for a, r in moves[:2]:
             move_scale_rows(a, r)
         up_raw = placed("up_raw", [P, PACK, N], F32, 172)
         nc.sync.dma_start(out=up_raw[:], in_=upw.rearrange("(p i) n -> p i n", i=PACK))
-        for a, r in moves[6:]:
+        for a, r in moves[2:]:
             move_scale_rows(a, r)
         dn_s = placed("dn_s", [P, PASSES, R], U8, 189)
         deal(dn_s[:], dn_raw_s[:], 16)
@@ -136,7 +137,7 @@ def tile_list_xcross_res_reluP_kernel(
             nc.vector.tensor_copy(out=w[:].bitcast(U16), in_=both[:].bitcast(U16).rearrange("p (j a) -> p a j", a=PASSES))
             v_w.append(w)
 
-        h_bf = [placed("h_bf%d" % h, [P, HALF, PACK], BF16, (1, 206)[h]) for h in range(HALVES)]
+        h_bf = [placed("h_bf%d" % h, [P, HALF, PACK], BF16, (172, 206)[h]) for h in range(HALVES)]
         h_w = [held("h_w%d" % h, [P, HALF], U32) for h in range(HALVES)]
         h_s = [held("h_s%d" % h, [P, HALF], U8) for h in range(HALVES)]
 
@@ -162,13 +163,12 @@ def tile_list_xcross_res_reluP_kernel(
         def quantize_hidden(h):
             nc.vector.quantize_mx(out=h_w[h][:].bitcast(FP8X4), scales=h_s[h][:], in_=h_bf[h][:].rearrange("p j i -> p (j i)"))
 
-        up_bf = held("up_bf", [P, N, PACK], BF16)
+        up_bf = placed("up_bf", [P, N, PACK], BF16, 214)
         for piece in range(UP_PIECES):
             ms = slice(piece * P // UP_PIECES, (piece + 1) * P // UP_PIECES)
-            nc.gpsimd.tensor_scalar(
+            nc.scalar.copy(
                 out=up_bf[:].rearrange("p (t m) i -> p m t i", t=PACK)[:, ms],
-                in0=up_raw[:].rearrange("p i (m t) -> p m t i", t=PACK)[:, ms],
-                scalar1=1.0, scalar2=0.0, op0=ALU.mult, op1=ALU.add,
+                in_=up_raw[:].rearrange("p i (m t) -> p m t i", t=PACK)[:, ms],
             )
         gather_words(0)
         hidden_half(0)
@@ -185,7 +185,7 @@ def tile_list_xcross_res_reluP_kernel(
         up_w = held("up_w", [P, N], U32)
         up_s = held("up_s", [P, N], U8)
         nc.vector.quantize_mx(out=up_w[:].bitcast(FP8X4), scales=up_s[:], in_=up_bf[:].rearrange("p n i -> p (n i)"))
-        wb4_s = placed("wb4_s", [P, PASSES, N], U8, 0)
+        wb4_s = placed("wb4_s", [P, PASSES, N], U8, 214)
         deal(wb4_s[:], wb4_raw_s[:], 16)
 
         pair = [held("pair%d" % u, [P, 2, J], F32) for u in range(2)]
@@ -195,22 +195,22 @@ def tile_list_xcross_res_reluP_kernel(
         def y_sum(t, h):
             cols = slice(t * P, (t + 1) * P)
             js = slice(h * HALF, (h + 1) * HALF)
-            y = psum.tile([P, HALF], F32, name="y", tag="bank")
+            acc = psum.tile([P, HALF], F32, name="y", tag="bank")
             for a in range(PASSES):
                 nc.tensor.matmul_mx(
-                    out=y[:], lhsT=wb8_w[:, a, cols].bitcast(FP8X4), lhsT_scale=wb8_s[:, a, cols],
+                    out=acc[:], lhsT=wb8_w[:, a, cols].bitcast(FP8X4), lhsT_scale=wb8_s[:, a, cols],
                     rhs=v_w[h][:, a, :].bitcast(FP4X4), rhs_scale=v_s[:, a, js], start=(a == 0), stop=False,
                 )
-            nc.tensor.matmul_mx(
-                out=y[:], lhsT=up_w[:, cols].bitcast(FP8X4), lhsT_scale=up_s[:, cols],
-                rhs=h_w[h][:].bitcast(FP8X4), rhs_scale=h_s[h][:], start=False, stop=False,
-            )
             for a in range(PASSES):
                 nc.tensor.matmul_mx(
-                    out=y[:], lhsT=wb4_w[:, a, 2 * t * P : 2 * (t + 1) * P].bitcast(FP4X4), lhsT_scale=wb4_s[:, a, cols],
-                    rhs=v_w[h][:, a, :].bitcast(FP4X4), rhs_scale=v_s[:, a, js], start=False, stop=(a == PASSES - 1),
+                    out=acc[:], lhsT=wb4_w[:, a, 2 * t * P : 2 * (t + 1) * P].bitcast(FP4X4), lhsT_scale=wb4_s[:, a, cols],
+                    rhs=v_w[h][:, a, :].bitcast(FP4X4), rhs_scale=v_s[:, a, js], start=False, stop=False,
                 )
-            return y
+            nc.tensor.matmul_mx(
+                out=acc[:], lhsT=up_w[:, cols].bitcast(FP8X4), lhsT_scale=up_s[:, cols],
+                rhs=h_w[h][:].bitcast(FP8X4), rhs_scale=h_s[h][:], start=False, stop=True,
+            )
+            return acc
 
         def round_pair(u, c):
             nc.scalar.copy(
@@ -222,7 +222,7 @@ def tile_list_xcross_res_reluP_kernel(
         y_last = held("y_last", [P, J], F32)
 
         def pick(t):
-            picked = placed("picked%d" % t, [P, J], F32, (2, 206, 198)[t])
+            picked = placed("picked%d" % t, [P, J], F32, (172, 206, 198)[t])
             for h in range(HALVES):
                 nc.vector.tensor_copy(
                     out=picked[:, h * HALF : (h + 1) * HALF], in_=x0[t][:].indirect(listed(h * HALF, HALF))
@@ -233,21 +233,22 @@ def tile_list_xcross_res_reluP_kernel(
             for h in range(HALVES):
                 js = slice(h * HALF, (h + 1) * HALF)
                 nc.vector.scalar_tensor_tensor(
-                    out=pair[t // 2][:, t % 2, js], in0=y_sum(t, h)[:], scalar=b1[:, t : t + 1], in1=picked[:, js],
+                    out=pair[t // 2][:, t % 2, js], in0=y[t, h][:], scalar=b1[:, t : t + 1], in1=picked[:, js],
                     op0=ALU.add, op1=ALU.mult,
                 )
 
         first = pick(0)
         quantize_hidden(1)
+        y = {(t, h): y_sum(t, h) for t, h in ((0, 0), (1, 0), (0, 1), (1, 1), (2, 0), (2, 1), (3, 0), (3, 1))}
         for t in range(2):
             cross(t, first if t == 0 else pick(t))
-            nc.sync.dma_start(out=out_rows[:, t, :], in_=pair[0][:, t, :])
+        nc.sync.dma_start(out=out_rows[:, 0:2, :], in_=pair[0][:])
         for c in range(len(CHUNKS)):
             round_pair(0, c)
         cross(2, pick(2))
         for h in range(HALVES):
             nc.scalar.activation(
-                out=y_last[:, h * HALF : (h + 1) * HALF], in_=y_sum(last, h)[:], func=ACT.Identity, bias=b1[:, last : last + 1]
+                out=y_last[:, h * HALF : (h + 1) * HALF], in_=y[last, h][:], func=ACT.Identity, bias=b1[:, last : last + 1]
             )
         nc.sync.dma_start(out=out_rows[:, 2, :], in_=pair[1][:, 0, :])
 
@@ -261,16 +262,15 @@ def tile_list_xcross_res_reluP_kernel(
                 op=ALU.mult,
             )
             round_pair(1, c)
-            if js.stop % HALF == 0:
-                half = slice(js.stop - HALF, js.stop)
-                nc.sync.dma_start(out=out_rows[:, last, half], in_=pair[1][:, 1, half])
+            if js.stop in STORED:
+                nc.sync.dma_start(out=out_rows[:, last, STORED[js.stop]], in_=pair[1][:, 1, STORED[js.stop]])
         for c, js in enumerate(CHUNKS):
             nc.vector.quantize_mx(
                 out=out_w[:, js].bitcast(FP8X4), scales=out_s[:, js], in_=out_bf[c][:].rearrange("p j i -> p (j i)")
             )
-            if js.stop % HALF == 0:
-                half = slice(js.stop - HALF, js.stop)
-                nc.sync.dma_start(out=words_out[:, half], in_=out_w[:, half].bitcast(I32))
+            if js.stop in STORED:
+                queue = nc.scalar if js.stop == J else nc.sync
+                queue.dma_start(out=words_out[:, STORED[js.stop]], in_=out_w[:, STORED[js.stop]].bitcast(I32))
         for r in range(4):
-            queue = nc.sync if r % 2 == 0 else nc.scalar
+            queue = nc.sync if r < 3 else nc.scalar
             queue.dma_start(out=out_2[0, r::4, :].bitcast(I32), in_=out_s[r:P:32, :].bitcast(I32))

@@ -22,8 +22,8 @@ PASSES = K // (P * PACK)
 HALF = 512
 HALVES = J // HALF
 HCHUNK = 128
-CHUNKS = (slice(0, 256), slice(256, 512), slice(512, 768), slice(768, 896), slice(896, 1024))
-STORED = {512: slice(0, 512), 896: slice(512, 896), 1024: slice(896, 1024)}
+CHUNKS = (slice(0, 256), slice(256, 512), slice(512, 768), slice(768, 1024))
+STORED = {512: slice(0, 512), 768: slice(512, 768), 1024: slice(768, 1024)}
 LIST_ROWS = 16
 UP_PIECES = 1
 
@@ -213,43 +213,33 @@ def tile_list_xcross_res_reluP_kernel(
             return acc
 
         def round_pair(u, c):
-            nc.scalar.copy(
+            copy = nc.vector.tensor_copy if u == 0 or c == len(CHUNKS) - 1 else nc.scalar.copy
+            copy(
                 out=out_bf[c][:, :, 2 * u : 2 * u + 2],
                 in_=pair[u][:, :, CHUNKS[c]].rearrange("p e j -> p j e"),
             )
 
         last = PACK - 1
-        y_last = held("y_last", [P, J], F32)
+        biased = [held("biased%d" % t, [P, J], F32) for t in range(PACK)]
 
-        def pick(t):
-            picked = placed("picked%d" % t, [P, J], F32, (172, 206, 198)[t])
-            for h in range(HALVES):
-                nc.vector.tensor_copy(
-                    out=picked[:, h * HALF : (h + 1) * HALF], in_=x0[t][:].indirect(listed(h * HALF, HALF))
-                )
-            return picked
-
-        def cross(t, picked):
-            for h in range(HALVES):
-                js = slice(h * HALF, (h + 1) * HALF)
-                nc.vector.scalar_tensor_tensor(
-                    out=pair[t // 2][:, t % 2, js], in0=y[t, h][:], scalar=b1[:, t : t + 1], in1=picked[:, js],
-                    op0=ALU.add, op1=ALU.mult,
-                )
-
-        first = pick(0)
-        quantize_hidden(1)
-        y = {(t, h): y_sum(t, h) for t, h in ((0, 0), (1, 0), (0, 1), (1, 1), (2, 0), (2, 1), (3, 0), (3, 1))}
-        for t in range(2):
-            cross(t, first if t == 0 else pick(t))
-        nc.sync.dma_start(out=out_rows[:, 0:2, :], in_=pair[0][:])
-        for c in range(len(CHUNKS)):
-            round_pair(0, c)
-        cross(2, pick(2))
-        for h in range(HALVES):
-            nc.scalar.activation(
-                out=y_last[:, h * HALF : (h + 1) * HALF], in_=y[last, h][:], func=ACT.Identity, bias=b1[:, last : last + 1]
+        def cross(t, js):
+            nc.vector.tensor_tensor(
+                out=pair[t // 2][:, t % 2, js], in0=x0[t][:].indirect(listed(js.start, js.stop - js.start)),
+                in1=biased[t][:, js], op=ALU.mult,
             )
+
+        quantize_hidden(1)
+        for t, h in ((0, 0), (1, 0), (0, 1), (1, 1), (2, 0), (2, 1), (3, 0), (3, 1)):
+            nc.scalar.activation(
+                out=biased[t][:, h * HALF : (h + 1) * HALF], in_=y_sum(t, h)[:], func=ACT.Identity, bias=b1[:, t : t + 1]
+            )
+        for t in range(last):
+            for h in range(HALVES):
+                cross(t, slice(h * HALF, (h + 1) * HALF))
+            if t == 1:
+                nc.sync.dma_start(out=out_rows[:, 0:2, :], in_=pair[0][:])
+                for c in range(len(CHUNKS)):
+                    round_pair(0, c)
         nc.sync.dma_start(out=out_rows[:, 2, :], in_=pair[1][:, 0, :])
 
         out_w = held("out_w", [P, J], U32)
@@ -257,13 +247,11 @@ def tile_list_xcross_res_reluP_kernel(
         words_out = out_1[0].rearrange("p j f -> p (j f)").bitcast(I32)
 
         for c, js in enumerate(CHUNKS):
-            nc.vector.tensor_tensor(
-                out=pair[1][:, 1, js], in0=x0[last][:].indirect(listed(js.start, js.stop - js.start)), in1=y_last[:, js],
-                op=ALU.mult,
-            )
+            cross(last, js)
             round_pair(1, c)
-            if js.stop in STORED:
-                nc.sync.dma_start(out=out_rows[:, last, STORED[js.stop]], in_=pair[1][:, 1, STORED[js.stop]])
+            if js.stop % HALF == 0:
+                half = slice(js.stop - HALF, js.stop)
+                nc.sync.dma_start(out=out_rows[:, last, half], in_=pair[1][:, 1, half])
         for c, js in enumerate(CHUNKS):
             nc.vector.quantize_mx(
                 out=out_w[:, js].bitcast(FP8X4), scales=out_s[:, js], in_=out_bf[c][:].rearrange("p j i -> p (j i)")

@@ -25,7 +25,9 @@ HCHUNK = 128
 CHUNKS = (slice(0, 256), slice(256, 512), slice(512, 768), slice(768, 1024))
 STORED = {512: slice(0, 512), 768: slice(512, 768), 1024: slice(768, 1024)}
 LIST_ROWS = 16
-UP_PIECES = 1
+STAGE = 96
+SCALE_ROWS = 32
+DN, WB8, WB4 = range(3)
 
 
 def tile_list_xcross_res_reluP_kernel(
@@ -41,103 +43,90 @@ def tile_list_xcross_res_reluP_kernel(
         def held(name, shape, dtype):
             return keep.tile(shape, dtype, name=name, align_bytes=64)
 
-        def placed(name, shape, dtype, unit):
-            return reuse.tile(shape, dtype, name=name, align_bytes=64, offset=unit * 512)
+        def placed(name, shape, dtype, offset):
+            return reuse.tile(shape, dtype, name=name, align_bytes=64, offset=offset)
 
         def listed(j0, n):
             return offsets[:, j0 // LIST_ROWS : (j0 + n) // LIST_ROWS]
 
-        def load_scale_rows(queue, plane, scales):
-            for r in range(4):
-                queue.dma_start(
-                    out=plane[r:P:32].bitcast(I32),
-                    in_=scales.rearrange("a (q r) c -> r q a c", r=4)[r].bitcast(I32),
-                )
-
         def deal(out, in_, run):
             nc.vector.tensor_copy(
-                out=out.rearrange("p a (t c i) -> p a c t i", t=PACK, i=run),
-                in_=in_.rearrange("p a (c i t) -> p a c t i", t=PACK, i=run),
+                out=out.rearrange("p a (t c i) -> p c a t i", t=PACK, i=run),
+                in_=in_.rearrange("p a (c i t) -> p c a t i", t=PACK, i=run),
             )
 
-        def zero_planes(engine, tile):
-            engine.memset(tile[:].rearrange("p a c -> p (a c)").bitcast(I32), 0)
+        def zero_other_partitions(words):
+            nc.vector.memset(words[0:STAGE, :], 0)
+
+        staged_rows = slice(STAGE, STAGE + SCALE_ROWS)
 
         offsets = keep.tile([P, J // LIST_ROWS], U16, name="offsets")
         nc.sync.dma_start(offsets[:], offs)
 
-        b_raw = reuse.tile([P, 32], F32, name="b_raw", align_bytes=64, offset=40 * 512 - 64)
-        nc.sync.dma_start(out=b_raw[:, 0:PACK], in_=b.rearrange("(p t) -> p t", t=PACK))
-        b1 = held("b1", [P, PACK], F32)
-        nc.vector.tensor_scalar_add(out=b1[:], in0=b_raw[:, 0:PACK], scalar1=1.0)
+        tab_s = placed("tab_s", [P, T // 4], I32, 0)
+        nc.sync.dma_start(out=tab_s[staged_rows, :], in_=tab_scales.rearrange("a q t -> (a q) t").bitcast(I32))
+        zero_other_partitions(tab_s)
+        raw_s = placed("raw_s", [P, 3 * N // 4], I32, T)
+        for w, scales in ((DN, dn_scales), (WB8, wb8_scales), (WB4, wb4_scales)):
+            nc.sync.dma_start(
+                out=raw_s[staged_rows, w * N // 4 : (w + 1) * N // 4], in_=scales.rearrange("a q c -> (a q) c").bitcast(I32)
+            )
+        zero_other_partitions(raw_s)
+
+        b_raw = held("b_raw", [P, PACK], F32)
+
 
         dn_raw = held("dn_raw", [P, PASSES, R], I32)
         nc.sync.dma_start(out=dn_raw[:], in_=dn_words.rearrange("a p r f -> p a (r f)").bitcast(I32))
-        wb8_raw = held("wb8_raw", [P, PASSES, N], I32)
-        nc.sync.dma_start(out=wb8_raw[:], in_=wb8_words.rearrange("a p n f -> p a (n f)").bitcast(I32))
-        tab_s = placed("tab_s", [P, T], U8, 187)
-        nc.vector.memset(tab_s[:].bitcast(I32), 0)
-        nc.sync.dma_start(out=tab_s[0:P:4, :].bitcast(I32), in_=tab_scales.rearrange("a q t -> (a q) t").bitcast(I32))
-        dn_raw_s = placed("dn_raw_s", [P, PASSES, R], U8, 103)
-        zero_planes(nc.vector, dn_raw_s)
-        load_scale_rows(nc.sync, dn_raw_s, dn_scales)
-        wb8_raw_s = held("wb8_raw_s", [P, PASSES, N], U8)
-        zero_planes(nc.gpsimd, wb8_raw_s)
-        wb4_raw_s = held("wb4_raw_s", [P, PASSES, N], U8)
-        zero_planes(nc.gpsimd, wb4_raw_s)
-        load_scale_rows(nc.gpsimd, wb8_raw_s, wb8_scales)
-        load_scale_rows(nc.gpsimd, wb4_raw_s, wb4_scales)
-        v_s = held("v_s", [P, PASSES, J], U8)
-        zero_planes(nc.vector, v_s)
-        wb4_raw = placed("wb4_raw", [P, PASSES, 2 * N], U8, 36)
-        nc.sync.dma_start(out=wb4_raw[:].bitcast(I32), in_=wb4_words.rearrange("a p c -> p a c").bitcast(I32))
-        tab_w = placed("tab_w", [P, T], I32, 40)
+        tab_w = held("tab_w", [P, T], I32)
         nc.sync.dma_start(out=tab_w[:], in_=tab_words[0].rearrange("p t f -> p (t f)").bitcast(I32))
 
         picked_s = held("picked_s", [P, J], U8)
-        nc.vector.tensor_copy(out=picked_s[:], in_=tab_s[:].indirect(offsets[:]))
-        dn_w = held("dn_w", [P, PASSES, R], I32)
-        deal(dn_w[:], dn_raw[:], 4)
+        nc.vector.tensor_copy(out=picked_s[:], in_=tab_s[:].bitcast(U8).indirect(offsets[:]))
+        staged = held("staged", [P, J + 3 * N], U8)
+        deal(staged[:, J:].rearrange("p (w c) -> p w c", w=3), raw_s[:].bitcast(U8).rearrange("p (w c) -> p w c", w=3), 16)
+        nc.vector.tensor_copy(out=staged[:, 0:J].bitcast(I32), in_=picked_s[:].bitcast(I32))
+
+        planes = placed("planes", [P, PASSES, J + 3 * N], U8, 0)
 
         def move_scale_rows(a, r):
-            nc.sync.dma_start(
-                out=v_s[r:P:32, a, :].bitcast(I32), in_=picked_s[64 * a + 4 * r : 64 * (a + 1) : 16, :].bitcast(I32)
-            )
+            first = STAGE + 16 * a + r
+            nc.sync.dma_start(out=planes[r:P:32, a, :].bitcast(I32), in_=staged[first : first + 13 : 4, :].bitcast(I32))
+
+        def weight_scales(w, a, t):
+            return planes[:, a, J + w * N + t * P : J + w * N + (t + 1) * P]
 
         moves = [(a, r) for a in range(PASSES) for r in range(4)]
-        for a, r in moves[:2]:
+        for a, r in moves[:6]:
             move_scale_rows(a, r)
-        up_raw = placed("up_raw", [P, PACK, N], F32, 172)
+        wb8_raw = held("wb8_raw", [P, PASSES, N], I32)
+        nc.sync.dma_start(out=wb8_raw[:], in_=wb8_words.rearrange("a p n f -> p a (n f)").bitcast(I32))
+        for a, r in moves[6:]:
+            move_scale_rows(a, r)
+        up_raw = held("up_raw", [P, PACK, N], F32)
         nc.sync.dma_start(out=up_raw[:], in_=upw.rearrange("(p i) n -> p i n", i=PACK))
-        for a, r in moves[2:]:
-            move_scale_rows(a, r)
-        dn_s = placed("dn_s", [P, PASSES, R], U8, 189)
-        deal(dn_s[:], dn_raw_s[:], 16)
-        wb4_w = placed("wb4_w", [P, PASSES, 2 * N], U8, 194)
-        deal(wb4_w[:].bitcast(U16), wb4_raw[:].bitcast(U16), 8)
-        wb8_w = placed("wb8_w", [P, PASSES, N], I32, 96)
-        deal(wb8_w[:], wb8_raw[:], 4)
-
-        x0 = []
-
-        def load_x0(unit):
-            t = len(x0)
-            x0.append(placed("x0_%d" % t, [P, T], F32, unit))
+        wb4_raw = held("wb4_raw", [P, PASSES, 2 * N], U8)
+        nc.sync.dma_start(out=wb4_raw[:].bitcast(I32), in_=wb4_words.rearrange("a p c -> p a c").bitcast(I32))
+        nc.sync.dma_start(out=b_raw[:], in_=b.rearrange("(p t) -> p t", t=PACK))
+        x0 = [held("x0_%d" % t, [P, T], F32) for t in range(PACK)]
+        for t in range(PACK):
             nc.sync.dma_start(out=x0[t][:], in_=x0T.rearrange("(p t) c -> p t c", t=PACK)[:, t, :])
 
-        load_x0(104)
+        dn_w = held("dn_w", [P, PASSES, R], I32)
+        deal(dn_w[:], dn_raw[:], 4)
+        b1 = held("b1", [P, PACK], F32)
+        nc.scalar.activation(out=b1[:], in_=b_raw[:], func=ACT.Identity, bias=1.0)
 
         v_w = []
 
-
         def gather_words(h):
-            both = placed("both", [P, HALF], U32, 137)
+            both = held("both", [P, HALF], U32)
             nc.vector.tensor_copy(out=both[:], in_=tab_w[:].bitcast(U32).indirect(listed(h * HALF, HALF)))
             w = held("v_w%d" % h, [P, PASSES, 2 * HALF], U8)
             nc.vector.tensor_copy(out=w[:].bitcast(U16), in_=both[:].bitcast(U16).rearrange("p (j a) -> p a j", a=PASSES))
             v_w.append(w)
 
-        h_bf = [placed("h_bf%d" % h, [P, HALF, PACK], BF16, (172, 206)[h]) for h in range(HALVES)]
+        h_bf = [held("h_bf%d" % h, [P, HALF, PACK], BF16) for h in range(HALVES)]
         h_w = [held("h_w%d" % h, [P, HALF], U32) for h in range(HALVES)]
         h_s = [held("h_s%d" % h, [P, HALF], U8) for h in range(HALVES)]
 
@@ -150,9 +139,9 @@ def tile_list_xcross_res_reluP_kernel(
                         nc.tensor.matmul_mx(
                             out=hs[:, t, :],
                             lhsT=dn_w[:, a, t * P : (t + 1) * P].bitcast(FP8X4),
-                            lhsT_scale=dn_s[:, a, t * P : (t + 1) * P],
+                            lhsT_scale=weight_scales(DN, a, t),
                             rhs=v_w[h][:, a, 2 * c * HCHUNK : 2 * (c + 1) * HCHUNK].bitcast(FP4X4),
-                            rhs_scale=v_s[:, a, j0 : j0 + HCHUNK],
+                            rhs_scale=planes[:, a, j0 : j0 + HCHUNK],
                             start=(a == PASSES - 1),
                             stop=(a == 0),
                         )
@@ -163,30 +152,24 @@ def tile_list_xcross_res_reluP_kernel(
         def quantize_hidden(h):
             nc.vector.quantize_mx(out=h_w[h][:].bitcast(FP8X4), scales=h_s[h][:], in_=h_bf[h][:].rearrange("p j i -> p (j i)"))
 
-        up_bf = placed("up_bf", [P, N, PACK], BF16, 214)
-        for piece in range(UP_PIECES):
-            ms = slice(piece * P // UP_PIECES, (piece + 1) * P // UP_PIECES)
-            nc.scalar.copy(
-                out=up_bf[:].rearrange("p (t m) i -> p m t i", t=PACK)[:, ms],
-                in_=up_raw[:].rearrange("p i (m t) -> p m t i", t=PACK)[:, ms],
-            )
         gather_words(0)
         hidden_half(0)
         gather_words(1)
-        load_x0(16)
-        load_x0(64)
-        load_x0(140)
         hidden_half(1)
 
-        wb8_s = placed("wb8_s", [P, PASSES, N], U8, 136)
-        deal(wb8_s[:], wb8_raw_s[:], 16)
-
+        wb8_w = held("wb8_w", [P, PASSES, N], I32)
+        deal(wb8_w[:], wb8_raw[:], 4)
+        up_bf = held("up_bf", [P, N, PACK], BF16)
+        nc.vector.tensor_copy(
+            out=up_bf[:].rearrange("p (t m) i -> p m t i", t=PACK), in_=up_raw[:].rearrange("p i (m t) -> p m t i", t=PACK)
+        )
         quantize_hidden(0)
         up_w = held("up_w", [P, N], U32)
         up_s = held("up_s", [P, N], U8)
         nc.vector.quantize_mx(out=up_w[:].bitcast(FP8X4), scales=up_s[:], in_=up_bf[:].rearrange("p n i -> p (n i)"))
-        wb4_s = placed("wb4_s", [P, PASSES, N], U8, 214)
-        deal(wb4_s[:], wb4_raw_s[:], 16)
+        wb4_w = held("wb4_w", [P, PASSES, 2 * N], U8)
+        deal(wb4_w[:].bitcast(U16), wb4_raw[:].bitcast(U16), 8)
+        quantize_hidden(1)
 
         pair = [held("pair%d" % u, [P, 2, J], F32) for u in range(2)]
         out_bf = [held("out_bf%d" % c, [P, js.stop - js.start, PACK], BF16) for c, js in enumerate(CHUNKS)]
@@ -198,13 +181,13 @@ def tile_list_xcross_res_reluP_kernel(
             acc = psum.tile([P, HALF], F32, name="y", tag="bank")
             for a in range(PASSES):
                 nc.tensor.matmul_mx(
-                    out=acc[:], lhsT=wb8_w[:, a, cols].bitcast(FP8X4), lhsT_scale=wb8_s[:, a, cols],
-                    rhs=v_w[h][:, a, :].bitcast(FP4X4), rhs_scale=v_s[:, a, js], start=(a == 0), stop=False,
+                    out=acc[:], lhsT=wb4_w[:, a, 2 * t * P : 2 * (t + 1) * P].bitcast(FP4X4), lhsT_scale=weight_scales(WB4, a, t),
+                    rhs=v_w[h][:, a, :].bitcast(FP4X4), rhs_scale=planes[:, a, js], start=(a == 0), stop=False,
                 )
             for a in range(PASSES):
                 nc.tensor.matmul_mx(
-                    out=acc[:], lhsT=wb4_w[:, a, 2 * t * P : 2 * (t + 1) * P].bitcast(FP4X4), lhsT_scale=wb4_s[:, a, cols],
-                    rhs=v_w[h][:, a, :].bitcast(FP4X4), rhs_scale=v_s[:, a, js], start=False, stop=False,
+                    out=acc[:], lhsT=wb8_w[:, a, cols].bitcast(FP8X4), lhsT_scale=weight_scales(WB8, a, t),
+                    rhs=v_w[h][:, a, :].bitcast(FP4X4), rhs_scale=planes[:, a, js], start=False, stop=False,
                 )
             nc.tensor.matmul_mx(
                 out=acc[:], lhsT=up_w[:, cols].bitcast(FP8X4), lhsT_scale=up_s[:, cols],
@@ -212,8 +195,7 @@ def tile_list_xcross_res_reluP_kernel(
             )
             return acc
 
-        def round_pair(u, c):
-            copy = nc.vector.tensor_copy if u == 0 or c == len(CHUNKS) - 1 else nc.scalar.copy
+        def round_pair(u, c, copy):
             copy(
                 out=out_bf[c][:, :, 2 * u : 2 * u + 2],
                 in_=pair[u][:, :, CHUNKS[c]].rearrange("p e j -> p j e"),
@@ -228,18 +210,18 @@ def tile_list_xcross_res_reluP_kernel(
                 in1=biased[t][:, js], op=ALU.mult,
             )
 
-        quantize_hidden(1)
-        for t, h in ((0, 0), (1, 0), (0, 1), (1, 1), (2, 0), (2, 1), (3, 0), (3, 1)):
-            nc.scalar.activation(
-                out=biased[t][:, h * HALF : (h + 1) * HALF], in_=y_sum(t, h)[:], func=ACT.Identity, bias=b1[:, t : t + 1]
-            )
+        for t in range(PACK):
+            for h in range(HALVES):
+                nc.scalar.activation(
+                    out=biased[t][:, h * HALF : (h + 1) * HALF], in_=y_sum(t, h)[:], func=ACT.Identity, bias=b1[:, t : t + 1]
+                )
         for t in range(last):
             for h in range(HALVES):
                 cross(t, slice(h * HALF, (h + 1) * HALF))
             if t == 1:
                 nc.sync.dma_start(out=out_rows[:, 0:2, :], in_=pair[0][:])
                 for c in range(len(CHUNKS)):
-                    round_pair(0, c)
+                    round_pair(0, c, nc.vector.tensor_copy)
         nc.sync.dma_start(out=out_rows[:, 2, :], in_=pair[1][:, 0, :])
 
         out_w = held("out_w", [P, J], U32)
@@ -248,7 +230,7 @@ def tile_list_xcross_res_reluP_kernel(
 
         for c, js in enumerate(CHUNKS):
             cross(last, js)
-            round_pair(1, c)
+            round_pair(1, c, nc.vector.tensor_copy if c == len(CHUNKS) - 1 else nc.scalar.copy)
             if js.stop % HALF == 0:
                 half = slice(js.stop - HALF, js.stop)
                 nc.sync.dma_start(out=out_rows[:, last, half], in_=pair[1][:, 1, half])

@@ -25,8 +25,7 @@ HCHUNK = 128
 CHUNKS = (slice(0, 256), slice(256, 512), slice(512, 768), slice(768, 1024))
 STORED = {512: slice(0, 512), 768: slice(512, 768), 1024: slice(768, 1024)}
 LIST_ROWS = 16
-STAGE = 96
-SCALE_ROWS = 32
+STAGE_STEP = 4
 DN, WB8, WB4 = range(3)
 
 
@@ -55,25 +54,24 @@ def tile_list_xcross_res_reluP_kernel(
                 in_=in_.rearrange("p a (c i t) -> p c a t i", t=PACK, i=run),
             )
 
-        def zero_other_partitions(words):
-            nc.vector.memset(words[0:STAGE, :], 0)
-
-        staged_rows = slice(STAGE, STAGE + SCALE_ROWS)
+        staged_rows = slice(0, P, STAGE_STEP)
 
         offsets = keep.tile([P, J // LIST_ROWS], U16, name="offsets")
         nc.sync.dma_start(offsets[:], offs)
 
+        wb4_raw = held("wb4_raw", [P, PASSES, 2 * N], U8)
+        nc.sync.dma_start(out=wb4_raw[:].bitcast(I32), in_=wb4_words.rearrange("a p c -> p a c").bitcast(I32))
+        b_raw = held("b_raw", [P, PACK], F32)
+        nc.sync.dma_start(out=b_raw[:], in_=b.rearrange("(p t) -> p t", t=PACK))
         tab_s = placed("tab_s", [P, T // 4], I32, 0)
+        nc.vector.memset(tab_s[:], 0)
         nc.sync.dma_start(out=tab_s[staged_rows, :], in_=tab_scales.rearrange("a q t -> (a q) t").bitcast(I32))
-        zero_other_partitions(tab_s)
         raw_s = placed("raw_s", [P, 3 * N // 4], I32, T)
+        nc.vector.memset(raw_s[:], 0)
         for w, scales in ((DN, dn_scales), (WB8, wb8_scales), (WB4, wb4_scales)):
             nc.sync.dma_start(
                 out=raw_s[staged_rows, w * N // 4 : (w + 1) * N // 4], in_=scales.rearrange("a q c -> (a q) c").bitcast(I32)
             )
-        zero_other_partitions(raw_s)
-
-        b_raw = held("b_raw", [P, PACK], F32)
 
 
         dn_raw = held("dn_raw", [P, PASSES, R], I32)
@@ -90,30 +88,27 @@ def tile_list_xcross_res_reluP_kernel(
         planes = placed("planes", [P, PASSES, J + 3 * N], U8, 0)
 
         def move_scale_rows(a, r):
-            first = STAGE + 16 * a + r
-            nc.sync.dma_start(out=planes[r:P:32, a, :].bitcast(I32), in_=staged[first : first + 13 : 4, :].bitcast(I32))
+            first = STAGE_STEP * (16 * a + r)
+            nc.sync.dma_start(out=planes[r:P:32, a, :].bitcast(I32), in_=staged[first : first + 49 : 16, :].bitcast(I32))
 
         def weight_scales(w, a, t):
             return planes[:, a, J + w * N + t * P : J + w * N + (t + 1) * P]
 
-        moves = [(a, r) for a in range(PASSES) for r in range(4)]
-        for a, r in moves[:6]:
-            move_scale_rows(a, r)
-        wb8_raw = held("wb8_raw", [P, PASSES, N], I32)
-        nc.sync.dma_start(out=wb8_raw[:], in_=wb8_words.rearrange("a p n f -> p a (n f)").bitcast(I32))
-        for a, r in moves[6:]:
-            move_scale_rows(a, r)
+        for a in range(PASSES):
+            for r in range(4):
+                move_scale_rows(a, r)
         up_raw = held("up_raw", [P, PACK, N], F32)
         nc.sync.dma_start(out=up_raw[:], in_=upw.rearrange("(p i) n -> p i n", i=PACK))
-        wb4_raw = held("wb4_raw", [P, PASSES, 2 * N], U8)
-        nc.sync.dma_start(out=wb4_raw[:].bitcast(I32), in_=wb4_words.rearrange("a p c -> p a c").bitcast(I32))
-        nc.sync.dma_start(out=b_raw[:], in_=b.rearrange("(p t) -> p t", t=PACK))
+        wb8_raw = held("wb8_raw", [P, PASSES, N], I32)
+        nc.sync.dma_start(out=wb8_raw[:], in_=wb8_words.rearrange("a p n f -> p a (n f)").bitcast(I32))
         x0 = [held("x0_%d" % t, [P, T], F32) for t in range(PACK)]
         for t in range(PACK):
             nc.sync.dma_start(out=x0[t][:], in_=x0T.rearrange("(p t) c -> p t c", t=PACK)[:, t, :])
 
         dn_w = held("dn_w", [P, PASSES, R], I32)
         deal(dn_w[:], dn_raw[:], 4)
+        wb4_w = held("wb4_w", [P, PASSES, 2 * N], U8)
+        deal(wb4_w[:].bitcast(U16), wb4_raw[:].bitcast(U16), 8)
         b1 = held("b1", [P, PACK], F32)
         nc.scalar.activation(out=b1[:], in_=b_raw[:], func=ACT.Identity, bias=1.0)
 
@@ -157,8 +152,6 @@ def tile_list_xcross_res_reluP_kernel(
         gather_words(1)
         hidden_half(1)
 
-        wb8_w = held("wb8_w", [P, PASSES, N], I32)
-        deal(wb8_w[:], wb8_raw[:], 4)
         up_bf = held("up_bf", [P, N, PACK], BF16)
         nc.vector.tensor_copy(
             out=up_bf[:].rearrange("p (t m) i -> p m t i", t=PACK), in_=up_raw[:].rearrange("p i (m t) -> p m t i", t=PACK)
@@ -167,8 +160,8 @@ def tile_list_xcross_res_reluP_kernel(
         up_w = held("up_w", [P, N], U32)
         up_s = held("up_s", [P, N], U8)
         nc.vector.quantize_mx(out=up_w[:].bitcast(FP8X4), scales=up_s[:], in_=up_bf[:].rearrange("p n i -> p (n i)"))
-        wb4_w = held("wb4_w", [P, PASSES, 2 * N], U8)
-        deal(wb4_w[:].bitcast(U16), wb4_raw[:].bitcast(U16), 8)
+        wb8_w = held("wb8_w", [P, PASSES, N], I32)
+        deal(wb8_w[:], wb8_raw[:], 4)
         quantize_hidden(1)
 
         pair = [held("pair%d" % u, [P, 2, J], F32) for u in range(2)]
@@ -181,12 +174,12 @@ def tile_list_xcross_res_reluP_kernel(
             acc = psum.tile([P, HALF], F32, name="y", tag="bank")
             for a in range(PASSES):
                 nc.tensor.matmul_mx(
-                    out=acc[:], lhsT=wb4_w[:, a, 2 * t * P : 2 * (t + 1) * P].bitcast(FP4X4), lhsT_scale=weight_scales(WB4, a, t),
+                    out=acc[:], lhsT=wb8_w[:, a, cols].bitcast(FP8X4), lhsT_scale=weight_scales(WB8, a, t),
                     rhs=v_w[h][:, a, :].bitcast(FP4X4), rhs_scale=planes[:, a, js], start=(a == 0), stop=False,
                 )
             for a in range(PASSES):
                 nc.tensor.matmul_mx(
-                    out=acc[:], lhsT=wb8_w[:, a, cols].bitcast(FP8X4), lhsT_scale=weight_scales(WB8, a, t),
+                    out=acc[:], lhsT=wb4_w[:, a, 2 * t * P : 2 * (t + 1) * P].bitcast(FP4X4), lhsT_scale=weight_scales(WB4, a, t),
                     rhs=v_w[h][:, a, :].bitcast(FP4X4), rhs_scale=planes[:, a, js], start=False, stop=False,
                 )
             nc.tensor.matmul_mx(

@@ -59,27 +59,27 @@ def tile_list_xcross_res_reluP_kernel(
         offsets = keep.tile([P, J // LIST_ROWS], U16, name="offsets")
         nc.sync.dma_start(offsets[:], offs)
 
-        wb4_raw = held("wb4_raw", [P, PASSES, 2 * N], U8)
-        nc.sync.dma_start(out=wb4_raw[:].bitcast(I32), in_=wb4_words.rearrange("a p c -> p a c").bitcast(I32))
         b_raw = held("b_raw", [P, PACK], F32)
         nc.sync.dma_start(out=b_raw[:], in_=b.rearrange("(p t) -> p t", t=PACK))
-        tab_s = placed("tab_s", [P, T // 4], I32, 0)
-        nc.vector.memset(tab_s[:], 0)
-        nc.sync.dma_start(out=tab_s[staged_rows, :], in_=tab_scales.rearrange("a q t -> (a q) t").bitcast(I32))
+        wb4_raw = held("wb4_raw", [P, PASSES, 2 * N], U8)
+        nc.sync.dma_start(out=wb4_raw[:].bitcast(I32), in_=wb4_words.rearrange("a p c -> p a c").bitcast(I32))
         raw_s = placed("raw_s", [P, 3 * N // 4], I32, T)
-        nc.vector.memset(raw_s[:], 0)
+        nc.gpsimd.memset(raw_s[:], 0)
         for w, scales in ((DN, dn_scales), (WB8, wb8_scales), (WB4, wb4_scales)):
             nc.sync.dma_start(
                 out=raw_s[staged_rows, w * N // 4 : (w + 1) * N // 4], in_=scales.rearrange("a q c -> (a q) c").bitcast(I32)
             )
 
 
+        tab_s = placed("tab_s", [P, T // 4], I32, 0)
+        nc.vector.memset(tab_s[:], 0)
+        nc.sync.dma_start(out=tab_s[staged_rows, :], in_=tab_scales.rearrange("a q t -> (a q) t").bitcast(I32))
         dn_raw = held("dn_raw", [P, PASSES, R], I32)
         nc.sync.dma_start(out=dn_raw[:], in_=dn_words.rearrange("a p r f -> p a (r f)").bitcast(I32))
         tab_w = held("tab_w", [P, T], I32)
         nc.sync.dma_start(out=tab_w[:], in_=tab_words[0].rearrange("p t f -> p (t f)").bitcast(I32))
 
-        picked_s = held("picked_s", [P, J], U8)
+        picked_s = placed("picked_s", [P, J], U8, T + 3 * N)
         nc.vector.tensor_copy(out=picked_s[:], in_=tab_s[:].bitcast(U8).indirect(offsets[:]))
         staged = held("staged", [P, J + 3 * N], U8)
         deal(staged[:, J:].rearrange("p (w c) -> p w c", w=3), raw_s[:].bitcast(U8).rearrange("p (w c) -> p w c", w=3), 16)
@@ -94,11 +94,13 @@ def tile_list_xcross_res_reluP_kernel(
         def weight_scales(w, a, t):
             return planes[:, a, J + w * N + t * P : J + w * N + (t + 1) * P]
 
-        for a in range(PASSES):
-            for r in range(4):
-                move_scale_rows(a, r)
+        moves = [(a, r) for a in range(PASSES) for r in range(4)]
+        for a, r in moves[:6]:
+            move_scale_rows(a, r)
         up_raw = held("up_raw", [P, PACK, N], F32)
         nc.sync.dma_start(out=up_raw[:], in_=upw.rearrange("(p i) n -> p i n", i=PACK))
+        for a, r in moves[6:]:
+            move_scale_rows(a, r)
         wb8_raw = held("wb8_raw", [P, PASSES, N], I32)
         nc.sync.dma_start(out=wb8_raw[:], in_=wb8_words.rearrange("a p n f -> p a (n f)").bitcast(I32))
         x0 = [held("x0_%d" % t, [P, T], F32) for t in range(PACK)]
@@ -107,7 +109,7 @@ def tile_list_xcross_res_reluP_kernel(
 
         dn_w = held("dn_w", [P, PASSES, R], I32)
         deal(dn_w[:], dn_raw[:], 4)
-        wb4_w = held("wb4_w", [P, PASSES, 2 * N], U8)
+        wb4_w = placed("wb4_w", [P, PASSES, 2 * N], U8, T + 3 * N)
         deal(wb4_w[:].bitcast(U16), wb4_raw[:].bitcast(U16), 8)
         b1 = held("b1", [P, PACK], F32)
         nc.scalar.activation(out=b1[:], in_=b_raw[:], func=ACT.Identity, bias=1.0)

@@ -37,7 +37,7 @@ def tile_list_xcross_res_reluP_kernel(
     with ExitStack() as ctx:
         keep = ctx.enter_context(tc.tile_pool(name="keep", bufs=1))
         reuse = ctx.enter_context(tc.tile_pool(name="reuse", bufs=1))
-        psum = ctx.enter_context(tc.psum_pool(name="psum", bufs=8))
+        psum = ctx.enter_context(tc.psum_pool(name="psum", bufs=4))
 
         def held(name, shape, dtype):
             return keep.tile(shape, dtype, name=name, align_bytes=64)
@@ -74,10 +74,10 @@ def tile_list_xcross_res_reluP_kernel(
         tab_s = placed("tab_s", [P, T // 4], I32, 0)
         nc.vector.memset(tab_s[:], 0)
         nc.sync.dma_start(out=tab_s[staged_rows, :], in_=tab_scales.rearrange("a q t -> (a q) t").bitcast(I32))
-        dn_raw = held("dn_raw", [P, PASSES, R], I32)
-        nc.sync.dma_start(out=dn_raw[:], in_=dn_words.rearrange("a p r f -> p a (r f)").bitcast(I32))
         tab_w = held("tab_w", [P, T], I32)
         nc.sync.dma_start(out=tab_w[:], in_=tab_words[0].rearrange("p t f -> p (t f)").bitcast(I32))
+        dn_raw = placed("dn_raw", [P, PASSES, R], I32, 24576)
+        nc.sync.dma_start(out=dn_raw[:], in_=dn_words.rearrange("a p r f -> p a (r f)").bitcast(I32))
 
         picked_s = placed("picked_s", [P, J], U8, T + 3 * N)
         nc.vector.tensor_copy(out=picked_s[:], in_=tab_s[:].bitcast(U8).indirect(offsets[:]))
@@ -95,11 +95,11 @@ def tile_list_xcross_res_reluP_kernel(
             return planes[:, a, J + w * N + t * P : J + w * N + (t + 1) * P]
 
         moves = [(a, r) for a in range(PASSES) for r in range(4)]
-        for a, r in moves[:6]:
+        for a, r in moves[:4]:
             move_scale_rows(a, r)
         up_raw = held("up_raw", [P, PACK, N], F32)
         nc.sync.dma_start(out=up_raw[:], in_=upw.rearrange("(p i) n -> p i n", i=PACK))
-        for a, r in moves[6:]:
+        for a, r in moves[4:]:
             move_scale_rows(a, r)
         wb8_raw = held("wb8_raw", [P, PASSES, N], I32)
         nc.sync.dma_start(out=wb8_raw[:], in_=wb8_words.rearrange("a p n f -> p a (n f)").bitcast(I32))
@@ -119,7 +119,7 @@ def tile_list_xcross_res_reluP_kernel(
         def gather_words(h):
             both = held("both", [P, HALF], U32)
             nc.vector.tensor_copy(out=both[:], in_=tab_w[:].bitcast(U32).indirect(listed(h * HALF, HALF)))
-            w = held("v_w%d" % h, [P, PASSES, 2 * HALF], U8)
+            w = placed("v_w%d" % h, [P, PASSES, 2 * HALF], U8, 24576 + 2048 * h)
             nc.vector.tensor_copy(out=w[:].bitcast(U16), in_=both[:].bitcast(U16).rearrange("p (j a) -> p a j", a=PASSES))
             v_w.append(w)
 
@@ -127,32 +127,32 @@ def tile_list_xcross_res_reluP_kernel(
         h_w = [held("h_w%d" % h, [P, HALF], U32) for h in range(HALVES)]
         h_s = [held("h_s%d" % h, [P, HALF], U8) for h in range(HALVES)]
 
-        def hidden_half(h):
-            for c in range(HALF // HCHUNK):
-                hs = psum.tile([P, PACK, HCHUNK], F32, name="hs", tag="bank")
+        def hidden_half(h, steps):
+            banks = [psum.tile([P, PACK, HCHUNK], F32, name="hs") for c in range(HALF // HCHUNK)]
+            for a, c in steps:
                 j0 = h * HALF + c * HCHUNK
                 for t in range(PACK):
-                    for a in reversed(range(PASSES)):
-                        nc.tensor.matmul_mx(
-                            out=hs[:, t, :],
-                            lhsT=dn_w[:, a, t * P : (t + 1) * P].bitcast(FP8X4),
-                            lhsT_scale=weight_scales(DN, a, t),
-                            rhs=v_w[h][:, a, 2 * c * HCHUNK : 2 * (c + 1) * HCHUNK].bitcast(FP4X4),
-                            rhs_scale=planes[:, a, j0 : j0 + HCHUNK],
-                            start=(a == PASSES - 1),
-                            stop=(a == 0),
-                        )
-                nc.scalar.activation(
-                    out=h_bf[h][:, c * HCHUNK : (c + 1) * HCHUNK, :], in_=hs[:].rearrange("p t j -> p j t"), func=ACT.Relu
-                )
+                    nc.tensor.matmul_mx(
+                        out=banks[c][:, t, :],
+                        lhsT=dn_w[:, a, t * P : (t + 1) * P].bitcast(FP8X4),
+                        lhsT_scale=weight_scales(DN, a, t),
+                        rhs=v_w[h][:, a, 2 * c * HCHUNK : 2 * (c + 1) * HCHUNK].bitcast(FP4X4),
+                        rhs_scale=planes[:, a, j0 : j0 + HCHUNK],
+                        start=(a == 0 and t == 0),
+                        stop=(a == PASSES - 1 and t == PACK - 1),
+                    )
+                if a == PASSES - 1:
+                    nc.scalar.activation(
+                        out=h_bf[h][:, c * HCHUNK : (c + 1) * HCHUNK, :], in_=banks[c][:].rearrange("p t j -> p j t"), func=ACT.Relu
+                    )
 
         def quantize_hidden(h):
             nc.vector.quantize_mx(out=h_w[h][:].bitcast(FP8X4), scales=h_s[h][:], in_=h_bf[h][:].rearrange("p j i -> p (j i)"))
 
         gather_words(0)
-        hidden_half(0)
+        hidden_half(0, [(a, c) for a in range(PASSES) for c in range(HALF // HCHUNK)])
         gather_words(1)
-        hidden_half(1)
+        hidden_half(1, [(a, c) for c in range(HALF // HCHUNK) for a in range(PASSES)])
 
         up_bf = held("up_bf", [P, N, PACK], BF16)
         nc.vector.tensor_copy(
@@ -173,7 +173,7 @@ def tile_list_xcross_res_reluP_kernel(
         def y_sum(t, h):
             cols = slice(t * P, (t + 1) * P)
             js = slice(h * HALF, (h + 1) * HALF)
-            acc = psum.tile([P, HALF], F32, name="y", tag="bank")
+            acc = psum.tile([P, HALF], F32, name="y")
             for a in range(PASSES):
                 nc.tensor.matmul_mx(
                     out=acc[:], lhsT=wb8_w[:, a, cols].bitcast(FP8X4), lhsT_scale=weight_scales(WB8, a, t),
@@ -197,18 +197,18 @@ def tile_list_xcross_res_reluP_kernel(
             )
 
         last = PACK - 1
-        biased = [held("biased%d" % t, [P, J], F32) for t in range(PACK)]
+        biased = [[placed("biased%d_%d" % (t, h), [P, HALF], F32, 8192 + 2048 * (2 * t + h)) for h in range(HALVES)] for t in range(PACK)]
 
         def cross(t, js):
             nc.vector.tensor_tensor(
                 out=pair[t // 2][:, t % 2, js], in0=x0[t][:].indirect(listed(js.start, js.stop - js.start)),
-                in1=biased[t][:, js], op=ALU.mult,
+                in1=biased[t][js.start // HALF][:, js.start % HALF : js.start % HALF + js.stop - js.start], op=ALU.mult,
             )
 
         for t in range(PACK):
             for h in range(HALVES):
                 nc.scalar.activation(
-                    out=biased[t][:, h * HALF : (h + 1) * HALF], in_=y_sum(t, h)[:], func=ACT.Identity, bias=b1[:, t : t + 1]
+                    out=biased[t][h][:], in_=y_sum(t, h)[:], func=ACT.Identity, bias=b1[:, t : t + 1]
                 )
         for t in range(last):
             for h in range(HALVES):

@@ -25,6 +25,8 @@ HCHUNK = 128
 CHUNKS = (slice(0, 256), slice(256, 512), slice(512, 768), slice(768, 1024))
 STORED = {512: slice(0, 512), 768: slice(512, 768), 1024: slice(768, 1024)}
 LIST_ROWS = 16
+BIASED = (8192, 10240, 12288, 14336, 29696, 33792, 20480, 22528)
+OUT_BF = (28672, 30720, 32768, 34816)
 STAGE_STEP = 4
 DN, WB8, WB4 = range(3)
 
@@ -167,7 +169,7 @@ def tile_list_xcross_res_reluP_kernel(
         quantize_hidden(1)
 
         pair = [held("pair%d" % u, [P, 2, J], F32) for u in range(2)]
-        out_bf = [held("out_bf%d" % c, [P, js.stop - js.start, PACK], BF16) for c, js in enumerate(CHUNKS)]
+        out_bf = []
         out_rows = out_0.rearrange("(p t) j -> p t j", t=PACK)
 
         def y_sum(t, h):
@@ -197,7 +199,7 @@ def tile_list_xcross_res_reluP_kernel(
             )
 
         last = PACK - 1
-        biased = [[placed("biased%d_%d" % (t, h), [P, HALF], F32, 8192 + 2048 * (2 * t + h)) for h in range(HALVES)] for t in range(PACK)]
+        biased = [[placed("biased%d_%d" % (t, h), [P, HALF], F32, BIASED[2 * t + h]) for h in range(HALVES)] for t in range(PACK)]
 
         def cross(t, js):
             nc.vector.tensor_tensor(
@@ -215,9 +217,11 @@ def tile_list_xcross_res_reluP_kernel(
                 cross(t, slice(h * HALF, (h + 1) * HALF))
             if t == 1:
                 nc.sync.dma_start(out=out_rows[:, 0:2, :], in_=pair[0][:])
-                for c in range(len(CHUNKS)):
-                    round_pair(0, c, nc.vector.tensor_copy)
         nc.sync.dma_start(out=out_rows[:, 2, :], in_=pair[1][:, 0, :])
+
+        for c, js in enumerate(CHUNKS):
+            out_bf.append(placed("out_bf%d" % c, [P, js.stop - js.start, PACK], BF16, OUT_BF[c]))
+            round_pair(0, c, nc.scalar.copy)
 
         out_w = held("out_w", [P, J], U32)
         out_s = held("out_s", [P, J], U8)

@@ -26,7 +26,6 @@ CHUNKS = (slice(0, 256), slice(256, 512), slice(512, 768), slice(768, 1024))
 STORED = {512: slice(0, 512), 768: slice(512, 768), 1024: slice(768, 1024)}
 LIST_ROWS = 16
 BIASED = (8192, 10240, 12288, 14336, 29696, 33792, 20480, 22528)
-OUT_BF = (28672, 30720, 32768, 34816)
 STAGE_STEP = 4
 DN, WB8, WB4 = range(3)
 
@@ -58,15 +57,15 @@ def tile_list_xcross_res_reluP_kernel(
 
         staged_rows = slice(0, P, STAGE_STEP)
 
+        dn_raw = placed("dn_raw", [P, PASSES, R], I32, 24576)
+        nc.sync.dma_start(out=dn_raw[:], in_=dn_words.rearrange("a p r f -> p a (r f)").bitcast(I32))
         offsets = keep.tile([P, J // LIST_ROWS], U16, name="offsets")
         nc.sync.dma_start(offsets[:], offs)
 
-        b_raw = held("b_raw", [P, PACK], F32)
-        nc.sync.dma_start(out=b_raw[:], in_=b.rearrange("(p t) -> p t", t=PACK))
-        wb4_raw = held("wb4_raw", [P, PASSES, 2 * N], U8)
-        nc.sync.dma_start(out=wb4_raw[:].bitcast(I32), in_=wb4_words.rearrange("a p c -> p a c").bitcast(I32))
         raw_s = placed("raw_s", [P, 3 * N // 4], I32, T)
         nc.gpsimd.memset(raw_s[:], 0)
+        b_raw = held("b_raw", [P, PACK], F32)
+        nc.gpsimd.dma_start(out=b_raw[:], in_=b.rearrange("(p t) -> p t", t=PACK))
         for w, scales in ((DN, dn_scales), (WB8, wb8_scales), (WB4, wb4_scales)):
             nc.sync.dma_start(
                 out=raw_s[staged_rows, w * N // 4 : (w + 1) * N // 4], in_=scales.rearrange("a q c -> (a q) c").bitcast(I32)
@@ -78,8 +77,10 @@ def tile_list_xcross_res_reluP_kernel(
         nc.sync.dma_start(out=tab_s[staged_rows, :], in_=tab_scales.rearrange("a q t -> (a q) t").bitcast(I32))
         tab_w = held("tab_w", [P, T], I32)
         nc.sync.dma_start(out=tab_w[:], in_=tab_words[0].rearrange("p t f -> p (t f)").bitcast(I32))
-        dn_raw = placed("dn_raw", [P, PASSES, R], I32, 24576)
-        nc.sync.dma_start(out=dn_raw[:], in_=dn_words.rearrange("a p r f -> p a (r f)").bitcast(I32))
+        wb8_raw = held("wb8_raw", [P, PASSES, N], I32)
+        nc.sync.dma_start(out=wb8_raw[:], in_=wb8_words.rearrange("a p n f -> p a (n f)").bitcast(I32))
+        wb4_raw = held("wb4_raw", [P, PASSES, 2 * N], U8)
+        nc.sync.dma_start(out=wb4_raw[:].bitcast(I32), in_=wb4_words.rearrange("a p c -> p a c").bitcast(I32))
 
         picked_s = placed("picked_s", [P, J], U8, T + 3 * N)
         nc.vector.tensor_copy(out=picked_s[:], in_=tab_s[:].bitcast(U8).indirect(offsets[:]))
@@ -97,22 +98,18 @@ def tile_list_xcross_res_reluP_kernel(
             return planes[:, a, J + w * N + t * P : J + w * N + (t + 1) * P]
 
         moves = [(a, r) for a in range(PASSES) for r in range(4)]
-        for a, r in moves[:4]:
+        for a, r in moves[:5]:
             move_scale_rows(a, r)
         up_raw = held("up_raw", [P, PACK, N], F32)
         nc.sync.dma_start(out=up_raw[:], in_=upw.rearrange("(p i) n -> p i n", i=PACK))
-        for a, r in moves[4:]:
+        for a, r in moves[5:]:
             move_scale_rows(a, r)
-        wb8_raw = held("wb8_raw", [P, PASSES, N], I32)
-        nc.sync.dma_start(out=wb8_raw[:], in_=wb8_words.rearrange("a p n f -> p a (n f)").bitcast(I32))
         x0 = [held("x0_%d" % t, [P, T], F32) for t in range(PACK)]
         for t in range(PACK):
             nc.sync.dma_start(out=x0[t][:], in_=x0T.rearrange("(p t) c -> p t c", t=PACK)[:, t, :])
 
-        dn_w = held("dn_w", [P, PASSES, R], I32)
+        dn_w = placed("dn_w", [P, PASSES, R], I32, T + 3 * N)
         deal(dn_w[:], dn_raw[:], 4)
-        wb4_w = placed("wb4_w", [P, PASSES, 2 * N], U8, T + 3 * N)
-        deal(wb4_w[:].bitcast(U16), wb4_raw[:].bitcast(U16), 8)
         b1 = held("b1", [P, PACK], F32)
         nc.scalar.activation(out=b1[:], in_=b_raw[:], func=ACT.Identity, bias=1.0)
 
@@ -166,6 +163,8 @@ def tile_list_xcross_res_reluP_kernel(
         nc.vector.quantize_mx(out=up_w[:].bitcast(FP8X4), scales=up_s[:], in_=up_bf[:].rearrange("p n i -> p (n i)"))
         wb8_w = held("wb8_w", [P, PASSES, N], I32)
         deal(wb8_w[:], wb8_raw[:], 4)
+        wb4_w = held("wb4_w", [P, PASSES, 2 * N], U8)
+        deal(wb4_w[:].bitcast(U16), wb4_raw[:].bitcast(U16), 8)
         quantize_hidden(1)
 
         pair = [held("pair%d" % u, [P, 2, J], F32) for u in range(2)]
@@ -220,7 +219,7 @@ def tile_list_xcross_res_reluP_kernel(
         nc.sync.dma_start(out=out_rows[:, 2, :], in_=pair[1][:, 0, :])
 
         for c, js in enumerate(CHUNKS):
-            out_bf.append(placed("out_bf%d" % c, [P, js.stop - js.start, PACK], BF16, OUT_BF[c]))
+            out_bf.append(held("out_bf%d" % c, [P, js.stop - js.start, PACK], BF16))
             round_pair(0, c, nc.scalar.copy)
 
         out_w = held("out_w", [P, J], U32)
@@ -229,11 +228,14 @@ def tile_list_xcross_res_reluP_kernel(
 
         for c, js in enumerate(CHUNKS):
             cross(last, js)
-            round_pair(1, c, nc.vector.tensor_copy if c == len(CHUNKS) - 1 else nc.scalar.copy)
+            if c < len(CHUNKS) - 1:
+                round_pair(1, c, nc.scalar.copy)
             if js.stop % HALF == 0:
                 half = slice(js.stop - HALF, js.stop)
                 nc.sync.dma_start(out=out_rows[:, last, half], in_=pair[1][:, 1, half])
         for c, js in enumerate(CHUNKS):
+            if c == 1:
+                round_pair(1, len(CHUNKS) - 1, nc.vector.tensor_copy)
             nc.vector.quantize_mx(
                 out=out_w[:, js].bitcast(FP8X4), scales=out_s[:, js], in_=out_bf[c][:].rearrange("p j i -> p (j i)")
             )

@@ -41,10 +41,10 @@ def tile_list_xcross_res_reluP_kernel(
         psum = ctx.enter_context(tc.psum_pool(name="psum", bufs=4))
 
         def held(name, shape, dtype):
-            return keep.tile(shape, dtype, name=name, align_bytes=64)
+            return keep.tile(shape, dtype, name=name, align_bytes=256)
 
         def placed(name, shape, dtype, offset):
-            return reuse.tile(shape, dtype, name=name, align_bytes=64, offset=offset)
+            return reuse.tile(shape, dtype, name=name, align_bytes=256, offset=offset)
 
         def listed(j0, n):
             return offsets[:, j0 // LIST_ROWS : (j0 + n) // LIST_ROWS]

from contextlib import ExitStack

import concourse.mybir as mybir

K, R, N, T, J = 1024, 512, 512, 4096, 1024
FLOPS = 2 * J * (K * R + 2 * K * N + R * N)

F32 = mybir.dt.float32
BF16 = mybir.dt.bfloat16
I32 = mybir.dt.int32
U32 = mybir.dt.uint32
U16 = mybir.dt.uint16
U8 = mybir.dt.uint8
FP8X4 = mybir.dt.float8_e4m3fn_x4
FP4X4 = mybir.dt.float4_e2m1fn_x4
ACT = mybir.ActivationFunctionType
ALU = mybir.AluOpType

P = 128
PACK = 4
PASSES = K // (P * PACK)
HALF = 512
HALVES = J // HALF
HCHUNK = 128
CHUNKS = (slice(0, 256), slice(256, 512), slice(512, 768), slice(768, 1024))
STORED = {512: slice(0, 512), 768: slice(512, 768), 1024: slice(768, 1024)}
LIST_ROWS = 16
BIASED = (8192, 10240, 12288, 14336, 29696, 33792, 20480, 22528)
STAGE_STEP = 4
DN, WB8, WB4 = range(3)


def tile_list_xcross_res_reluP_kernel(
    tc, tab_words, tab_scales, wb4_words, wb4_scales, wb8_words, wb8_scales, dn_words, dn_scales, upw, x0T, b, offs,
    out_0, out_1, out_2,
):
    nc = tc.nc
    with ExitStack() as ctx:
        keep = ctx.enter_context(tc.tile_pool(name="keep", bufs=1))
        reuse = ctx.enter_context(tc.tile_pool(name="reuse", bufs=1))
        psum = ctx.enter_context(tc.psum_pool(name="psum", bufs=4))

        def held(name, shape, dtype):
            return keep.tile(shape, dtype, name=name, align_bytes=256)

        def placed(name, shape, dtype, offset):
            return reuse.tile(shape, dtype, name=name, align_bytes=256, offset=offset)

        def listed(j0, n):
            return offsets[:, j0 // LIST_ROWS : (j0 + n) // LIST_ROWS]

        def deal(out, in_, run):
            nc.vector.tensor_copy(
                out=out.rearrange("p a (t c i) -> p c a t i", t=PACK, i=run),
                in_=in_.rearrange("p a (c i t) -> p c a t i", t=PACK, i=run),
            )

        staged_rows = slice(0, P, STAGE_STEP)

        dn_raw = placed("dn_raw", [P, PASSES, R], I32, 24576)
        nc.sync.dma_start(out=dn_raw[:], in_=dn_words.rearrange("a p r f -> p a (r f)").bitcast(I32))
        offsets = keep.tile([P, J // LIST_ROWS], U16, name="offsets")
        nc.sync.dma_start(offsets[:], offs)

        raw_s = placed("raw_s", [P, 3 * N // 4], I32, T)
        nc.gpsimd.memset(raw_s[:], 0)
        b_raw = held("b_raw", [P, PACK], F32)
        nc.gpsimd.dma_start(out=b_raw[:], in_=b.rearrange("(p t) -> p t", t=PACK))
        for w, scales in ((DN, dn_scales), (WB8, wb8_scales), (WB4, wb4_scales)):
            nc.sync.dma_start(
                out=raw_s[staged_rows, w * N // 4 : (w + 1) * N // 4], in_=scales.rearrange("a q c -> (a q) c").bitcast(I32)
            )


        tab_s = placed("tab_s", [P, T // 4], I32, 0)
        nc.vector.memset(tab_s[:], 0)
        nc.sync.dma_start(out=tab_s[staged_rows, :], in_=tab_scales.rearrange("a q t -> (a q) t").bitcast(I32))
        tab_w = held("tab_w", [P, T], I32)
        nc.sync.dma_start(out=tab_w[:], in_=tab_words[0].rearrange("p t f -> p (t f)").bitcast(I32))
        wb8_raw = held("wb8_raw", [P, PASSES, N], I32)
        nc.sync.dma_start(out=wb8_raw[:], in_=wb8_words.rearrange("a p n f -> p a (n f)").bitcast(I32))
        wb4_raw = held("wb4_raw", [P, PASSES, 2 * N], U8)
        nc.sync.dma_start(out=wb4_raw[:].bitcast(I32), in_=wb4_words.rearrange("a p c -> p a c").bitcast(I32))

        picked_s = placed("picked_s", [P, J], U8, T + 3 * N)
        nc.vector.tensor_copy(out=picked_s[:], in_=tab_s[:].bitcast(U8).indirect(offsets[:]))
        staged = held("staged", [P, J + 3 * N], U8)
        deal(staged[:, J:].rearrange("p (w c) -> p w c", w=3), raw_s[:].bitcast(U8).rearrange("p (w c) -> p w c", w=3), 16)
        nc.vector.tensor_copy(out=staged[:, 0:J].bitcast(I32), in_=picked_s[:].bitcast(I32))

        planes = placed("planes", [P, PASSES, J + 3 * N], U8, 0)

        def move_scale_rows(a, r):
            first = STAGE_STEP * (16 * a + r)
            nc.sync.dma_start(out=planes[r:P:32, a, :].bitcast(I32), in_=staged[first : first + 49 : 16, :].bitcast(I32))

        def weight_scales(w, a, t):
            return planes[:, a, J + w * N + t * P : J + w * N + (t + 1) * P]

        moves = [(a, r) for a in range(PASSES) for r in range(4)]
        for a, r in moves[:5]:
            move_scale_rows(a, r)
        up_raw = held("up_raw", [P, PACK, N], F32)
        nc.sync.dma_start(out=up_raw[:], in_=upw.rearrange("(p i) n -> p i n", i=PACK))
        for a, r in moves[5:]:
            move_scale_rows(a, r)
        x0 = [held("x0_%d" % t, [P, T], F32) for t in range(PACK)]
        for t in range(PACK):
            nc.sync.dma_start(out=x0[t][:], in_=x0T.rearrange("(p t) c -> p t c", t=PACK)[:, t, :])

        dn_w = placed("dn_w", [P, PASSES, R], I32, T + 3 * N)
        deal(dn_w[:], dn_raw[:], 4)
        b1 = held("b1", [P, PACK], F32)
        nc.scalar.activation(out=b1[:], in_=b_raw[:], func=ACT.Identity, bias=1.0)

        v_w = []

        def gather_words(h):
            both = held("both", [P, HALF], U32)
            nc.vector.tensor_copy(out=both[:], in_=tab_w[:].bitcast(U32).indirect(listed(h * HALF, HALF)))
            w = placed("v_w%d" % h, [P, PASSES, 2 * HALF], U8, 24576 + 2048 * h)
            nc.vector.tensor_copy(out=w[:].bitcast(U16), in_=both[:].bitcast(U16).rearrange("p (j a) -> p a j", a=PASSES))
            v_w.append(w)

        h_bf = [held("h_bf%d" % h, [P, HALF, PACK], BF16) for h in range(HALVES)]
        h_w = [held("h_w%d" % h, [P, HALF], U32) for h in range(HALVES)]
        h_s = [held("h_s%d" % h, [P, HALF], U8) for h in range(HALVES)]

        def hidden_half(h, steps):
            banks = [psum.tile([P, PACK, HCHUNK], F32, name="hs") for c in range(HALF // HCHUNK)]
            for a, c in steps:
                j0 = h * HALF + c * HCHUNK
                for t in range(PACK):
                    nc.tensor.matmul_mx(
                        out=banks[c][:, t, :],
                        lhsT=dn_w[:, a, t * P : (t + 1) * P].bitcast(FP8X4),
                        lhsT_scale=weight_scales(DN, a, t),
                        rhs=v_w[h][:, a, 2 * c * HCHUNK : 2 * (c + 1) * HCHUNK].bitcast(FP4X4),
                        rhs_scale=planes[:, a, j0 : j0 + HCHUNK],
                        start=(a == 0 and t == 0),
                        stop=(a == PASSES - 1 and t == PACK - 1),
                    )
                if a == PASSES - 1:
                    nc.scalar.activation(
                        out=h_bf[h][:, c * HCHUNK : (c + 1) * HCHUNK, :], in_=banks[c][:].rearrange("p t j -> p j t"), func=ACT.Relu
                    )

        def quantize_hidden(h):
            nc.vector.quantize_mx(out=h_w[h][:].bitcast(FP8X4), scales=h_s[h][:], in_=h_bf[h][:].rearrange("p j i -> p (j i)"))

        gather_words(0)
        hidden_half(0, [(a, c) for a in range(PASSES) for c in range(HALF // HCHUNK)])
        gather_words(1)
        hidden_half(1, [(a, c) for c in range(HALF // HCHUNK) for a in range(PASSES)])

        up_bf = held("up_bf", [P, N, PACK], BF16)
        nc.vector.tensor_copy(
            out=up_bf[:].rearrange("p (t m) i -> p m t i", t=PACK), in_=up_raw[:].rearrange("p i (m t) -> p m t i", t=PACK)
        )
        quantize_hidden(0)
        up_w = held("up_w", [P, N], U32)
        up_s = held("up_s", [P, N], U8)
        nc.vector.quantize_mx(out=up_w[:].bitcast(FP8X4), scales=up_s[:], in_=up_bf[:].rearrange("p n i -> p (n i)"))
        wb8_w = held("wb8_w", [P, PASSES, N], I32)
        deal(wb8_w[:], wb8_raw[:], 4)
        wb4_w = held("wb4_w", [P, PASSES, 2 * N], U8)
        deal(wb4_w[:].bitcast(U16), wb4_raw[:].bitcast(U16), 8)
        quantize_hidden(1)

        pair = [held("pair%d" % u, [P, 2, J], F32) for u in range(2)]
        out_bf = []
        out_rows = out_0.rearrange("(p t) j -> p t j", t=PACK)

        def y_sum(t, h):
            cols = slice(t * P, (t + 1) * P)
            js = slice(h * HALF, (h + 1) * HALF)
            acc = psum.tile([P, HALF], F32, name="y")
            for a in range(PASSES):
                nc.tensor.matmul_mx(
                    out=acc[:], lhsT=wb8_w[:, a, cols].bitcast(FP8X4), lhsT_scale=weight_scales(WB8, a, t),
                    rhs=v_w[h][:, a, :].bitcast(FP4X4), rhs_scale=planes[:, a, js], start=(a == 0), stop=False,
                )
            for a in range(PASSES):
                nc.tensor.matmul_mx(
                    out=acc[:], lhsT=wb4_w[:, a, 2 * t * P : 2 * (t + 1) * P].bitcast(FP4X4), lhsT_scale=weight_scales(WB4, a, t),
                    rhs=v_w[h][:, a, :].bitcast(FP4X4), rhs_scale=planes[:, a, js], start=False, stop=False,
                )
            nc.tensor.matmul_mx(
                out=acc[:], lhsT=up_w[:, cols].bitcast(FP8X4), lhsT_scale=up_s[:, cols],
                rhs=h_w[h][:].bitcast(FP8X4), rhs_scale=h_s[h][:], start=False, stop=True,
            )
            return acc

        def round_pair(u, c, copy):
            copy(
                out=out_bf[c][:, :, 2 * u : 2 * u + 2],
                in_=pair[u][:, :, CHUNKS[c]].rearrange("p e j -> p j e"),
            )

        last = PACK - 1
        biased = [[placed("biased%d_%d" % (t, h), [P, HALF], F32, BIASED[2 * t + h]) for h in range(HALVES)] for t in range(PACK)]

        def cross(t, js):
            nc.vector.tensor_tensor(
                out=pair[t // 2][:, t % 2, js], in0=x0[t][:].indirect(listed(js.start, js.stop - js.start)),
                in1=biased[t][js.start // HALF][:, js.start % HALF : js.start % HALF + js.stop - js.start], op=ALU.mult,
            )

        for t in range(PACK):
            for h in range(HALVES):
                nc.scalar.activation(
                    out=biased[t][h][:], in_=y_sum(t, h)[:], func=ACT.Identity, bias=b1[:, t : t + 1]
                )
        for t in range(last):
            for h in range(HALVES):
                cross(t, slice(h * HALF, (h + 1) * HALF))
            if t == 1:
                nc.sync.dma_start(out=out_rows[:, 0:2, :], in_=pair[0][:])
        nc.sync.dma_start(out=out_rows[:, 2, :], in_=pair[1][:, 0, :])

        for c, js in enumerate(CHUNKS):
            out_bf.append(held("out_bf%d" % c, [P, js.stop - js.start, PACK], BF16))
            round_pair(0, c, nc.scalar.copy)

        out_w = held("out_w", [P, J], U32)
        out_s = held("out_s", [P, J], U8)
        words_out = out_1[0].rearrange("p j f -> p (j f)").bitcast(I32)

        for c, js in enumerate(CHUNKS):
            cross(last, js)
            if c < len(CHUNKS) - 1:
                round_pair(1, c, nc.scalar.copy)
            if js.stop % HALF == 0:
                half = slice(js.stop - HALF, js.stop)
                nc.sync.dma_start(out=out_rows[:, last, half], in_=pair[1][:, 1, half])
        for c, js in enumerate(CHUNKS):
            if c == 1:
                round_pair(1, len(CHUNKS) - 1, nc.vector.tensor_copy)
            nc.vector.quantize_mx(
                out=out_w[:, js].bitcast(FP8X4), scales=out_s[:, js], in_=out_bf[c][:].rearrange("p j i -> p (j i)")
            )
            if js.stop in STORED:
                queue = nc.scalar if js.stop == J else nc.sync
                queue.dma_start(out=words_out[:, STORED[js.stop]], in_=out_w[:, STORED[js.stop]].bitcast(I32))
        for r in range(4):
            queue = nc.sync if r < 3 else nc.scalar
            queue.dma_start(out=out_2[0, r::4, :].bitcast(I32), in_=out_s[r:P:32, :].bitcast(I32))
